import numpy as np
import ml_dtypes


def mxq(x, axis, fmt="e4m3"):
    dtype, down = {"e4m3": (ml_dtypes.float8_e4m3fn, 7), "e5m2": (ml_dtypes.float8_e5m2, 14)}[fmt]
    v = np.moveaxis(np.asarray(x, np.float32).astype(ml_dtypes.bfloat16).astype(np.float64), axis, -1)
    blocks = v.reshape(v.shape[:-1] + (-1, 32))
    amax = np.abs(blocks).max(-1, keepdims=True)
    byte = np.maximum(np.where(amax > 0, np.frexp(amax)[1] - 1 + 127, 0) - down, 1)
    scale = np.exp2(byte - 127.0)
    codes = (blocks / scale).astype(np.float32).astype(dtype).astype(np.float64)
    return np.moveaxis((codes * scale).reshape(v.shape), -1, axis)


WIDE = False


def mx_kscale(k):
    if not WIDE:
        return np.ones(k)
    levels = np.array([10, -10, 5, -5, 0])
    if k % 512:
        return np.exp2(np.random.permutation(np.resize(levels, k // 32))).repeat(32)
    a = np.empty((k // 512, 16))
    for p in range(k // 512):
        a[p, :8] = np.random.permutation(np.resize(levels, 8))
        for g in range(8):
            far = levels[np.abs(levels - a[p, g]) >= 10]
            a[p, g + 8] = far[np.random.randint(len(far))]
    return np.exp2(a.ravel()).repeat(32)


def f64(x):
    return np.asarray(x).astype(np.float64)


def striped(idx):
    return np.tile(idx.reshape(-1, 16).T, (8, 1)).astype(np.uint16)


def unstriped(offs):
    return offs[:16].T.reshape(-1).astype(np.int64)


def pack_weight(w):
    k, n = w.shape
    w = f64(np.asarray(w, np.float32).astype(ml_dtypes.bfloat16)).reshape(k // 32, 32, n)
    amax = np.abs(w).max(1)
    byte = np.clip(np.where(amax > 0, np.frexp(amax)[1] - 1 + 127 - 7, 1), 1, 254)
    scaled = (w * np.exp2(127.0 - byte)[:, None, :]).reshape(k, n).astype(np.float32)
    words = np.ascontiguousarray(scaled.reshape(k // 512, 128, 4, n).transpose(0, 1, 3, 2)).astype(ml_dtypes.float8_e4m3fn).view(np.uint8)
    return words, np.ascontiguousarray(byte.astype(np.uint8).reshape(k // 512, 16, n))


def unpack_weight(words, scales):
    g, p, n, _ = words.shape
    vals = np.ascontiguousarray(words).view(ml_dtypes.float8_e4m3fn).astype(np.float64) * np.repeat(np.exp2(scales.astype(np.float64) - 127.0), 8, axis=1)[..., None]
    return vals.transpose(0, 1, 3, 2).reshape(g * 512, n)


def silu(v):
    return v / (1.0 + np.exp(-np.maximum(v, -700.0)))


K, T, S, H, N, U = 512, 2048, 1024, 512, 256, 2048
P = 2 ** 7


def setup_inputs():
    n = np.random.standard_normal
    s = mx_kscale(K)[:, None]
    u = mx_kscale(H)
    packed_xT = pack_weight(n((K, T)) * s)
    packed_w2 = pack_weight(n((H, N)) / np.sqrt(H) / u[:, None])
    return {
        "x_words": packed_xT[0],
        "x_scales": packed_xT[1],
        "gate": np.tile(np.random.uniform(0.5, 1.5, S), (P, 1)).astype(np.float32),
        "w1": (n((K, H)) / np.sqrt(K) / s).astype(np.float32),
        "w3": (n((K, H)) / np.sqrt(K) / s * u).astype(np.float32),
        "w2_words": packed_w2[0],
        "w2_scales": packed_w2[1],
        "offs": striped(np.random.permutation(T)[:S]),
        "dst": striped(np.random.permutation(U)[:S]),
    }


def reference(x_words, x_scales, gate, w1, w3, w2_words, w2_scales, offs, dst):
    xq = unpack_weight(x_words, x_scales)[:, unstriped(offs)]
    h = (silu(mxq(f64(w1), 0, "e4m3").T @ xq)) * ((mxq(f64(w3), 0, "e4m3").T @ xq))
    y = unpack_weight(w2_words, w2_scales).T @ mxq(h, 0, "e4m3")
    out = np.zeros((N, U))
    out[:, unstriped(dst)] = y * f64(gate)[:1]
    return out

@@ -1,0 +1,158 @@
+from contextlib import ExitStack
+
+import concourse.mybir as mybir
+
+K, T, S, H, N, U = 512, 2048, 1024, 512, 256, 2048
+FLOPS = 2 * S * (2 * K * H + H * N)
+
+F32 = mybir.dt.float32
+BF16 = mybir.dt.bfloat16
+I32 = mybir.dt.int32
+U32 = mybir.dt.uint32
+U16 = mybir.dt.uint16
+U8 = mybir.dt.uint8
+FP8X4 = mybir.dt.float8_e4m3fn_x4
+MULT = mybir.AluOpType.mult
+SILU = mybir.ActivationFunctionType.Silu
+
+P = 128
+PACK = 4
+CHUNK = 128
+HALF = 512
+W_COLS = H // 2
+PER_COL = 16
+
+
+def load_scale_rows(queue, plane, rows):
+    for q in range(4):
+        queue.dma_start(out=plane[32 * q : 32 * q + 4, :].bitcast(I32), in_=rows[4 * q : 4 * q + 4, :].bitcast(I32))
+
+
+def tile_picked_route2_glusilu_p_kernel(
+    tc, x_words, x_scales, gate, w1, w3, w2_words, w2_scales, offs, dst, out
+):
+    nc = tc.nc
+    with ExitStack() as ctx:
+        keep = ctx.enter_context(tc.tile_pool(name="keep", bufs=1))
+        psum_a = ctx.enter_context(tc.psum_pool(name="psum_a", bufs=3))
+        psum_b = ctx.enter_context(tc.psum_pool(name="psum_b", bufs=3))
+        psum_y = ctx.enter_context(tc.psum_pool(name="psum_y", bufs=2))
+
+        offs_sb = keep.tile([P, S // PER_COL], U16, name="offs_sb")
+        dst_sb = keep.tile([P, S // PER_COL], U16, name="dst_sb")
+        xs_table = keep.tile([P, T], U8, name="xs_table", tag="scale_rows", align_bytes=64)
+        xw_table = keep.tile([P, T], U32, name="xw_table", align_bytes=64)
+        windows = [keep.tile([P, U], F32, name=f"window{m}", align_bytes=64) for m in range(N // P)]
+
+        nc.gpsimd.memset(xs_table[:].bitcast(I32), 0)
+        nc.sync.dma_start(offs_sb[:], offs)
+        nc.sync.dma_start(out=xw_table[:].bitcast(I32), in_=x_words[0].rearrange("p c r -> p (c r)").bitcast(I32))
+        load_scale_rows(nc.sync, xs_table, x_scales[0])
+        raw = {}
+        for name, w in (("w1", w1), ("w3", w3)):
+            for c in range(2):
+                raw[name, c] = keep.tile([P, PACK, W_COLS], F32, name=f"raw_{name}_{c}", tag=f"raw_{name}_{c}", align_bytes=64)
+                nc.sync.dma_start(
+                    out=raw[name, c][:],
+                    in_=w.rearrange("(p j) c -> p j c", j=PACK)[:, :, c * W_COLS : (c + 1) * W_COLS],
+                )
+        nc.sync.dma_start(dst_sb[:], dst)
+
+        nc.vector.memset(windows[0][:], 0.0)
+        nc.scalar.activation(windows[1][:], windows[0][:], SILU)
+
+        xs = keep.tile([P, S], U8, name="xs", align_bytes=64)
+        xw = keep.tile([P, S], U32, name="xw", align_bytes=64)
+        for g in range(S // HALF):
+            cols = slice(g * HALF // PER_COL, (g + 1) * HALF // PER_COL)
+            nc.vector.tensor_copy(xw[:, g * HALF : (g + 1) * HALF], xw_table[:].indirect(offs_sb[:, cols]))
+            nc.vector.tensor_copy(xs[:, g * HALF : (g + 1) * HALF], xs_table[:].indirect(offs_sb[:, cols]))
+
+        codes, scales = {}, {}
+        for name, copy in (("w1", nc.scalar.copy), ("w3", nc.vector.tensor_copy)):
+            grouped = keep.tile([P, H * PACK], BF16, name=f"grouped_{name}", align_bytes=64)
+            dealt = grouped[:].rearrange("p (t m j) -> p m j t", t=PACK, j=PACK)
+            for c in range(2):
+                m_cols = slice(c * P // 2, (c + 1) * P // 2)
+                copy(dealt[:, m_cols], raw[name, c][:].rearrange("p j (m t) -> p m j t", t=PACK))
+            codes[name] = keep.tile([P, H], U32, name=f"codes_{name}", align_bytes=64)
+            scales[name] = keep.tile([P, H], U8, name=f"scales_{name}", align_bytes=64)
+            nc.vector.quantize_mx(out=codes[name][:].bitcast(FP8X4), scales=scales[name][:], in_=grouped[:])
+
+        gate_sb = keep.tile([P, S], F32, name="gate_sb", tag="raw_w1_0", align_bytes=64)
+        nc.sync.dma_start(out=gate_sb[:], in_=gate)
+        w2w = keep.tile([P, N], U32, name="w2w", tag="raw_w1_1", align_bytes=64)
+        nc.sync.dma_start(out=w2w[:].bitcast(I32), in_=w2_words[0].rearrange("p c r -> p (c r)").bitcast(I32))
+        w2s = keep.tile([P, N], U8, name="w2s", tag="scale_rows", align_bytes=64)
+        nc.vector.memset(w2s[:].bitcast(I32), 0)
+        load_scale_rows(nc.sync, w2s, w2_scales[0])
+
+        def first_product(bank, name, c):
+            tokens = slice(c * CHUNK, (c + 1) * CHUNK)
+            for t in range(PACK):
+                cols = slice(t * P, (t + 1) * P)
+                nc.tensor.matmul_mx(
+                    out=bank[:, t, :],
+                    lhsT=codes[name][:, cols].bitcast(FP8X4),
+                    lhsT_scale=scales[name][:, cols],
+                    rhs=xw[:, tokens].bitcast(FP8X4),
+                    rhs_scale=xs[:, tokens],
+                    start=True,
+                    stop=True,
+                )
+
+        n_chunks = S // CHUNK
+        per_half = HALF // CHUNK
+        silu = []
+        for c in range(n_chunks):
+            bank_a = psum_a.tile([P, PACK, CHUNK], F32, name="bank_a")
+            first_product(bank_a, "w1", c)
+            silu.append(keep.tile([P, CHUNK, PACK], F32, name=f"silu{c}", align_bytes=64))
+            nc.scalar.activation(silu[c][:], bank_a[:].rearrange("p t n -> p n t"), SILU)
+
+        h = [keep.tile([P, HALF * PACK], BF16, name=f"h{g}", align_bytes=64) for g in range(S // HALF)]
+        y = {}
+
+        def multiply(c):
+            bank_b = psum_b.tile([P, PACK, CHUNK], F32, name="bank_b")
+            first_product(bank_b, "w3", c)
+            g, i = divmod(c, per_half)
+            part = h[g][:, i * CHUNK * PACK : (i + 1) * CHUNK * PACK].rearrange("p (n t) -> p n t", t=PACK)
+            nc.vector.tensor_tensor(part, bank_b[:].rearrange("p t n -> p n t"), silu[c][:], MULT)
+
+        def second_product(g):
+            hw = keep.tile([P, HALF], U32, name=f"hw{g}", align_bytes=64)
+            hs = keep.tile([P, HALF], U8, name=f"hs{g}", align_bytes=64)
+            nc.vector.quantize_mx(out=hw[:].bitcast(FP8X4), scales=hs[:], in_=h[g][:])
+            for m in range(N // P):
+                cols = slice(m * P, (m + 1) * P)
+                bank_y = psum_y.tile([P, HALF], F32, name="bank_y")
+                nc.tensor.matmul_mx(
+                    out=bank_y[:],
+                    lhsT=w2w[:, cols].bitcast(FP8X4),
+                    lhsT_scale=w2s[:, cols],
+                    rhs=hw[:].bitcast(FP8X4),
+                    rhs_scale=hs[:],
+                    start=True,
+                    stop=True,
+                )
+                y[g, m] = keep.tile([P, HALF], F32, name=f"y{g}_{m}", align_bytes=64)
+                nc.scalar.copy(y[g, m][:], bank_y[:])
+
+        def scatter(g, m):
+            cols = slice(g * HALF // PER_COL, (g + 1) * HALF // PER_COL)
+            nc.vector.tensor_tensor(
+                windows[m][:].indirect(dst_sb[:, cols]), y[g, m][:], gate_sb[:, g * HALF : (g + 1) * HALF], MULT
+            )
+
+        for c in range(per_half + 1):
+            multiply(c)
+        second_product(0)
+        for c in range(per_half + 1, n_chunks):
+            multiply(c)
+        scatter(0, 0)
+        second_product(1)
+        scatter(0, 1)
+        for m in range(N // P):
+            scatter(1, m)
+            nc.sync.dma_start(out=out[m * P : (m + 1) * P, :], in_=windows[m][:])

@@ -21,6 +21,9 @@ CHUNK = 128
 HALF = 512
 W_COLS = H // 2
 PER_COL = 16
+LATE = 256
+PAIR = 2
+AHEAD = 4
 
 
 def load_scale_rows(queue, plane, rows):
@@ -34,9 +37,7 @@ def tile_picked_route2_glusilu_p_kernel(
     nc = tc.nc
     with ExitStack() as ctx:
         keep = ctx.enter_context(tc.tile_pool(name="keep", bufs=1))
-        psum_a = ctx.enter_context(tc.psum_pool(name="psum_a", bufs=3))
-        psum_b = ctx.enter_context(tc.psum_pool(name="psum_b", bufs=3))
-        psum_y = ctx.enter_context(tc.psum_pool(name="psum_y", bufs=2))
+        psum = ctx.enter_context(tc.psum_pool(name="psum", bufs=1))
 
         offs_sb = keep.tile([P, S // PER_COL], U16, name="offs_sb")
         dst_sb = keep.tile([P, S // PER_COL], U16, name="dst_sb")
@@ -44,40 +45,55 @@ def tile_picked_route2_glusilu_p_kernel(
         xw_table = keep.tile([P, T], U32, name="xw_table", align_bytes=64)
         windows = [keep.tile([P, U], F32, name=f"window{m}", align_bytes=64) for m in range(N // P)]
 
-        nc.gpsimd.memset(xs_table[:].bitcast(I32), 0)
-        nc.sync.dma_start(offs_sb[:], offs)
-        nc.sync.dma_start(out=xw_table[:].bitcast(I32), in_=x_words[0].rearrange("p c r -> p (c r)").bitcast(I32))
-        load_scale_rows(nc.sync, xs_table, x_scales[0])
         raw = {}
-        for name, w in (("w1", w1), ("w3", w3)):
-            for c in range(2):
-                raw[name, c] = keep.tile([P, PACK, W_COLS], F32, name=f"raw_{name}_{c}", tag=f"raw_{name}_{c}", align_bytes=64)
-                nc.sync.dma_start(
-                    out=raw[name, c][:],
-                    in_=w.rearrange("(p j) c -> p j c", j=PACK)[:, :, c * W_COLS : (c + 1) * W_COLS],
-                )
+
+        def load_weight_half(name, w, c):
+            raw[name, c] = keep.tile([P, PACK, W_COLS], F32, name=f"raw_{name}_{c}", tag=f"raw_{name}_{c}", align_bytes=64)
+            nc.sync.dma_start(
+                out=raw[name, c][:],
+                in_=w.rearrange("(p j) c -> p j c", j=PACK)[:, :, c * W_COLS : (c + 1) * W_COLS],
+            )
+
+        nc.vector.memset(xs_table[:].bitcast(I32), 0)
+        nc.sync.dma_start(offs_sb[:], offs)
+        load_weight_half("w1", w1, 0)
+        load_scale_rows(nc.sync, xs_table, x_scales[0])
+        load_weight_half("w1", w1, 1)
+        nc.sync.dma_start(out=xw_table[:].bitcast(I32), in_=x_words[0].rearrange("p c r -> p (c r)").bitcast(I32))
+        load_weight_half("w3", w3, 0)
+        load_weight_half("w3", w3, 1)
         nc.sync.dma_start(dst_sb[:], dst)
 
-        nc.vector.memset(windows[0][:], 0.0)
-        nc.scalar.activation(windows[1][:], windows[0][:], SILU)
+        nc.vector.memset(windows[0][:, : U // 2], 0.0)
+        nc.scalar.activation(windows[1][:, : U // 2], windows[0][:, : U // 2], SILU)
+        for window in windows:
+            nc.vector.memset(window[:, U // 2 :], 0.0)
 
-        xs = keep.tile([P, S], U8, name="xs", align_bytes=64)
-        xw = keep.tile([P, S], U32, name="xw", align_bytes=64)
-        for g in range(S // HALF):
-            cols = slice(g * HALF // PER_COL, (g + 1) * HALF // PER_COL)
-            nc.vector.tensor_copy(xw[:, g * HALF : (g + 1) * HALF], xw_table[:].indirect(offs_sb[:, cols]))
-            nc.vector.tensor_copy(xs[:, g * HALF : (g + 1) * HALF], xs_table[:].indirect(offs_sb[:, cols]))
+        xw, xs = {}, {}
+
+        def gather(into, table, dtype, first, count, tag):
+            picked = keep.tile([P, count], dtype, name=tag + "_picked", tag=tag, align_bytes=64)
+            cols = slice(first // PER_COL, (first + count) // PER_COL)
+            nc.vector.tensor_copy(picked[:], table[:].indirect(offs_sb[:, cols]))
+            for c in range(count // CHUNK):
+                into[first // CHUNK + c] = picked[:, c * CHUNK : (c + 1) * CHUNK]
+
+        gather(xs, xs_table, U8, 0, S, "xs")
 
         codes, scales = {}, {}
-        for name, copy in (("w1", nc.scalar.copy), ("w3", nc.vector.tensor_copy)):
-            grouped = keep.tile([P, H * PACK], BF16, name=f"grouped_{name}", align_bytes=64)
+        for name, copies in (("w1", (nc.scalar.copy, nc.scalar.copy)), ("w3", (nc.scalar.copy, nc.vector.tensor_copy))):
+            grouped = keep.tile([P, H * PACK], BF16, name=f"grouped_{name}", tag=f"grouped_{name}", align_bytes=64)
             dealt = grouped[:].rearrange("p (t m j) -> p m j t", t=PACK, j=PACK)
             for c in range(2):
                 m_cols = slice(c * P // 2, (c + 1) * P // 2)
-                copy(dealt[:, m_cols], raw[name, c][:].rearrange("p j (m t) -> p m j t", t=PACK))
+                copies[c](dealt[:, m_cols], raw[name, c][:].rearrange("p j (m t) -> p m j t", t=PACK))
             codes[name] = keep.tile([P, H], U32, name=f"codes_{name}", align_bytes=64)
             scales[name] = keep.tile([P, H], U8, name=f"scales_{name}", align_bytes=64)
             nc.vector.quantize_mx(out=codes[name][:].bitcast(FP8X4), scales=scales[name][:], in_=grouped[:])
+            if name == "w1":
+                gather(xw, xw_table, U32, 0, LATE, "xw0")
+                gather(xw, xw_table, U32, LATE, S - 2 * LATE, "xw1")
+        gather(xw, xw_table, U32, S - LATE, LATE, "grouped_w3")
 
         gate_sb = keep.tile([P, S], F32, name="gate_sb", tag="raw_w1_0", align_bytes=64)
         nc.sync.dma_start(out=gate_sb[:], in_=gate)
@@ -88,37 +104,40 @@ def tile_picked_route2_glusilu_p_kernel(
         load_scale_rows(nc.sync, w2s, w2_scales[0])
 
         def first_product(bank, name, c):
-            tokens = slice(c * CHUNK, (c + 1) * CHUNK)
             for t in range(PACK):
                 cols = slice(t * P, (t + 1) * P)
                 nc.tensor.matmul_mx(
                     out=bank[:, t, :],
                     lhsT=codes[name][:, cols].bitcast(FP8X4),
                     lhsT_scale=scales[name][:, cols],
-                    rhs=xw[:, tokens].bitcast(FP8X4),
-                    rhs_scale=xs[:, tokens],
+                    rhs=xw[c].bitcast(FP8X4),
+                    rhs_scale=xs[c],
                     start=True,
                     stop=True,
                 )
 
         n_chunks = S // CHUNK
         per_half = HALF // CHUNK
-        silu = []
-        for c in range(n_chunks):
-            bank_a = psum_a.tile([P, PACK, CHUNK], F32, name="bank_a")
+        silu_tiles = [
+            keep.tile([P, per_half, CHUNK // PAIR, PACK, PAIR], F32, name=f"silu{g}", tag=tag, align_bytes=64)
+            for g, tag in enumerate(("raw_w3_0", "silu1"))
+        ]
+        silu = [silu_tiles[c // per_half][:, c % per_half] for c in range(n_chunks)]
+
+        def activate(c):
+            bank_a = psum.tile([P, PACK, CHUNK], F32, name="bank_a", tag=f"bank{c}")
             first_product(bank_a, "w1", c)
-            silu.append(keep.tile([P, CHUNK, PACK], F32, name=f"silu{c}", align_bytes=64))
-            nc.scalar.activation(silu[c][:], bank_a[:].rearrange("p t n -> p n t"), SILU)
+            nc.scalar.activation(silu[c], bank_a[:].rearrange("p t (n i) -> p n t i", i=PAIR), SILU)
 
         h = [keep.tile([P, HALF * PACK], BF16, name=f"h{g}", align_bytes=64) for g in range(S // HALF)]
         y = {}
 
         def multiply(c):
-            bank_b = psum_b.tile([P, PACK, CHUNK], F32, name="bank_b")
+            bank_b = psum.tile([P, PACK, CHUNK], F32, name="bank_b", tag=f"bank{(c + per_half) % n_chunks}")
             first_product(bank_b, "w3", c)
             g, i = divmod(c, per_half)
-            part = h[g][:, i * CHUNK * PACK : (i + 1) * CHUNK * PACK].rearrange("p (n t) -> p n t", t=PACK)
-            nc.vector.tensor_tensor(part, bank_b[:].rearrange("p t n -> p n t"), silu[c][:], MULT)
+            part = h[g][:, i * CHUNK * PACK : (i + 1) * CHUNK * PACK].rearrange("p (n i t) -> p n t i", t=PACK, i=PAIR)
+            nc.vector.tensor_tensor(part, bank_b[:].rearrange("p t (n i) -> p n t i", i=PAIR), silu[c], MULT)
 
         def second_product(g):
             hw = keep.tile([P, HALF], U32, name=f"hw{g}", align_bytes=64)
@@ -126,7 +145,7 @@ def tile_picked_route2_glusilu_p_kernel(
             nc.vector.quantize_mx(out=hw[:].bitcast(FP8X4), scales=hs[:], in_=h[g][:])
             for m in range(N // P):
                 cols = slice(m * P, (m + 1) * P)
-                bank_y = psum_y.tile([P, HALF], F32, name="bank_y")
+                bank_y = psum.tile([P, HALF], F32, name="bank_y", tag=f"bank{per_half + 2 * g + m}")
                 nc.tensor.matmul_mx(
                     out=bank_y[:],
                     lhsT=w2w[:, cols].bitcast(FP8X4),
@@ -145,11 +164,14 @@ def tile_picked_route2_glusilu_p_kernel(
                 windows[m][:].indirect(dst_sb[:, cols]), y[g, m][:], gate_sb[:, g * HALF : (g + 1) * HALF], MULT
             )
 
-        for c in range(per_half + 1):
+        for c in range(AHEAD):
+            activate(c)
+        for c in range(n_chunks):
             multiply(c)
-        second_product(0)
-        for c in range(per_half + 1, n_chunks):
-            multiply(c)
+            if c + AHEAD < n_chunks:
+                activate(c + AHEAD)
+            if c == per_half:
+                second_product(0)
         scatter(0, 0)
         second_product(1)
         scatter(0, 1)

@@ -19,7 +19,7 @@ P = 128
 PACK = 4
 CHUNK = 128
 HALF = 512
-W_COLS = H // 2
+PIECES = {"w1": (slice(0, H // 4), slice(H // 4, H)), "w3": (slice(0, H // 2), slice(H // 2, H))}
 PER_COL = 16
 LATE = 256
 PAIR = 2
@@ -48,11 +48,11 @@ def tile_picked_route2_glusilu_p_kernel(
         raw = {}
 
         def load_weight_half(name, w, c):
-            raw[name, c] = keep.tile([P, PACK, W_COLS], F32, name=f"raw_{name}_{c}", tag=f"raw_{name}_{c}", align_bytes=64)
-            nc.sync.dma_start(
-                out=raw[name, c][:],
-                in_=w.rearrange("(p j) c -> p j c", j=PACK)[:, :, c * W_COLS : (c + 1) * W_COLS],
+            cols = PIECES[name][c]
+            raw[name, c] = keep.tile(
+                [P, PACK, cols.stop - cols.start], F32, name=f"raw_{name}_{c}", tag=f"raw_{name}_{c}", align_bytes=64
             )
+            nc.sync.dma_start(out=raw[name, c][:], in_=w.rearrange("(p j) c -> p j c", j=PACK)[:, :, cols])
 
         nc.vector.memset(xs_table[:].bitcast(I32), 0)
         nc.sync.dma_start(offs_sb[:], offs)
@@ -64,10 +64,9 @@ def tile_picked_route2_glusilu_p_kernel(
         load_weight_half("w3", w3, 1)
         nc.sync.dma_start(dst_sb[:], dst)
 
-        nc.vector.memset(windows[0][:, : U // 2], 0.0)
-        nc.scalar.activation(windows[1][:, : U // 2], windows[0][:, : U // 2], SILU)
-        for window in windows:
-            nc.vector.memset(window[:, U // 2 :], 0.0)
+        for half in (slice(0, U // 2), slice(U // 2, U)):
+            nc.vector.memset(windows[0][:, half], 0.0)
+            nc.scalar.activation(windows[1][:, half], windows[0][:, half], SILU)
 
         xw, xs = {}, {}
 
@@ -80,24 +79,43 @@ def tile_picked_route2_glusilu_p_kernel(
 
         gather(xs, xs_table, U8, 0, S, "xs")
 
-        codes, scales = {}, {}
-        for name, copies in (("w1", (nc.scalar.copy, nc.scalar.copy)), ("w3", (nc.scalar.copy, nc.vector.tensor_copy))):
-            grouped = keep.tile([P, H * PACK], BF16, name=f"grouped_{name}", tag=f"grouped_{name}", align_bytes=64)
-            dealt = grouped[:].rearrange("p (t m j) -> p m j t", t=PACK, j=PACK)
-            for c in range(2):
-                m_cols = slice(c * P // 2, (c + 1) * P // 2)
-                copies[c](dealt[:, m_cols], raw[name, c][:].rearrange("p j (m t) -> p m j t", t=PACK))
+        codes, scales, grouped = {}, {}, {}
+        for name in ("w1", "w3"):
+            grouped[name] = keep.tile([P, H * PACK], BF16, name=f"grouped_{name}", tag=f"grouped_{name}", align_bytes=64)
             codes[name] = keep.tile([P, H], U32, name=f"codes_{name}", align_bytes=64)
             scales[name] = keep.tile([P, H], U8, name=f"scales_{name}", align_bytes=64)
-            nc.vector.quantize_mx(out=codes[name][:].bitcast(FP8X4), scales=scales[name][:], in_=grouped[:])
-            if name == "w1":
-                gather(xw, xw_table, U32, 0, LATE, "xw0")
-                gather(xw, xw_table, U32, LATE, S - 2 * LATE, "xw1")
+
+        def deal(copy, name, c, tiles):
+            dealt = grouped[name][:].rearrange("p (t m j) -> p m j t", t=PACK, j=PACK)
+            source = raw[name, c][:].rearrange("p j (m t) -> p m j t", t=PACK)
+            cols = PIECES[name][c]
+            copy(dealt[:, cols.start // PACK : cols.stop // PACK, :, tiles], source[:, :, :, tiles])
+
+        def quantise(name, tiles):
+            cols = slice(tiles.start * P, tiles.stop * P)
+            nc.vector.quantize_mx(
+                out=codes[name][:, cols].bitcast(FP8X4),
+                scales=scales[name][:, cols],
+                in_=grouped[name][:, cols.start * PACK : cols.stop * PACK],
+            )
+
+        all_tiles = slice(0, PACK)
+        tile_pairs = (slice(0, 2), slice(2, PACK))
+        deal(nc.scalar.copy, "w1", 0, all_tiles)
+        deal(nc.scalar.copy, "w1", 1, all_tiles)
+        quantise("w1", all_tiles)
+        gather(xw, xw_table, U32, 0, LATE, "xw0")
+        gather(xw, xw_table, U32, LATE, S - 2 * LATE, "xw1")
+        deal(nc.scalar.copy, "w3", 0, all_tiles)
+        for tiles in tile_pairs:
+            deal(nc.vector.tensor_copy, "w3", 1, tiles)
+        for tiles in tile_pairs:
+            quantise("w3", tiles)
         gather(xw, xw_table, U32, S - LATE, LATE, "grouped_w3")
 
-        gate_sb = keep.tile([P, S], F32, name="gate_sb", tag="raw_w1_0", align_bytes=64)
+        gate_sb = keep.tile([P, S], F32, name="gate_sb", tag="raw_w1_1", align_bytes=64)
         nc.sync.dma_start(out=gate_sb[:], in_=gate)
-        w2w = keep.tile([P, N], U32, name="w2w", tag="raw_w1_1", align_bytes=64)
+        w2w = keep.tile([P, N], U32, name="w2w", tag="raw_w1_0", align_bytes=64)
         nc.sync.dma_start(out=w2w[:].bitcast(I32), in_=w2_words[0].rearrange("p c r -> p (c r)").bitcast(I32))
         w2s = keep.tile([P, N], U8, name="w2s", tag="scale_rows", align_bytes=64)
         nc.vector.memset(w2s[:].bitcast(I32), 0)
@@ -119,7 +137,7 @@ def tile_picked_route2_glusilu_p_kernel(
         n_chunks = S // CHUNK
         per_half = HALF // CHUNK
         silu_tiles = [
-            keep.tile([P, per_half, CHUNK // PAIR, PACK, PAIR], F32, name=f"silu{g}", tag=tag, align_bytes=64)
+            keep.tile([P, per_half, CHUNK, PACK], F32, name=f"silu{g}", tag=tag, align_bytes=64)
             for g, tag in enumerate(("raw_w3_0", "silu1"))
         ]
         silu = [silu_tiles[c // per_half][:, c % per_half] for c in range(n_chunks)]
@@ -127,17 +145,17 @@ def tile_picked_route2_glusilu_p_kernel(
         def activate(c):
             bank_a = psum.tile([P, PACK, CHUNK], F32, name="bank_a", tag=f"bank{c}")
             first_product(bank_a, "w1", c)
-            nc.scalar.activation(silu[c], bank_a[:].rearrange("p t (n i) -> p n t i", i=PAIR), SILU)
+            nc.scalar.activation(silu[c], bank_a[:].rearrange("p t n -> p n t"), SILU)
 
         h = [keep.tile([P, HALF * PACK], BF16, name=f"h{g}", align_bytes=64) for g in range(S // HALF)]
         y = {}
 
         def multiply(c):
-            bank_b = psum.tile([P, PACK, CHUNK], F32, name="bank_b", tag=f"bank{(c + per_half) % n_chunks}")
+            bank_b = psum.tile([P, PACK, CHUNK], F32, name="bank_b", tag=f"bank{(c + AHEAD) % n_chunks}")
             first_product(bank_b, "w3", c)
             g, i = divmod(c, per_half)
-            part = h[g][:, i * CHUNK * PACK : (i + 1) * CHUNK * PACK].rearrange("p (n i t) -> p n t i", t=PACK, i=PAIR)
-            nc.vector.tensor_tensor(part, bank_b[:].rearrange("p t (n i) -> p n t i", i=PAIR), silu[c], MULT)
+            part = h[g][:, i * CHUNK * PACK : (i + 1) * CHUNK * PACK].rearrange("p (n t) -> p n t", t=PACK)
+            nc.vector.tensor_tensor(part, bank_b[:].rearrange("p t n -> p n t"), silu[c], MULT)
 
         def second_product(g):
             hw = keep.tile([P, HALF], U32, name=f"hw{g}", align_bytes=64)
@@ -145,7 +163,7 @@ def tile_picked_route2_glusilu_p_kernel(
             nc.vector.quantize_mx(out=hw[:].bitcast(FP8X4), scales=hs[:], in_=h[g][:])
             for m in range(N // P):
                 cols = slice(m * P, (m + 1) * P)
-                bank_y = psum.tile([P, HALF], F32, name="bank_y", tag=f"bank{per_half + 2 * g + m}")
+                bank_y = psum.tile([P, HALF], F32, name="bank_y", tag=f"bank{(AHEAD + 2 * g + m) % n_chunks}")
                 nc.tensor.matmul_mx(
                     out=bank_y[:],
                     lhsT=w2w[:, cols].bitcast(FP8X4),

@@ -17,13 +17,10 @@ SILU = mybir.ActivationFunctionType.Silu
 
 P = 128
 PACK = 4
-CHUNK = 128
-HALF = 512
-PIECES = {"w1": (slice(0, H // 4), slice(H // 4, H)), "w3": (slice(0, H // 2), slice(H // 2, H))}
-PER_COL = 16
-LATE = 256
 PAIR = 2
-AHEAD = 4
+CHUNK = 128
+GROUP = 256
+PER_COL = 16
 
 
 def load_scale_rows(queue, plane, rows):
@@ -39,160 +36,187 @@ def tile_picked_route2_glusilu_p_kernel(
         keep = ctx.enter_context(tc.tile_pool(name="keep", bufs=1))
         psum = ctx.enter_context(tc.psum_pool(name="psum", bufs=1))
 
+        def sbuf(name, columns, dtype, tag=None):
+            return keep.tile([P, columns], dtype, name=name, tag=tag or name, align_bytes=64)
+
         offs_sb = keep.tile([P, S // PER_COL], U16, name="offs_sb")
         dst_sb = keep.tile([P, S // PER_COL], U16, name="dst_sb")
-        xs_table = keep.tile([P, T], U8, name="xs_table", tag="scale_rows", align_bytes=64)
-        xw_table = keep.tile([P, T], U32, name="xw_table", align_bytes=64)
-        windows = [keep.tile([P, U], F32, name=f"window{m}", align_bytes=64) for m in range(N // P)]
+        xs_table = sbuf("xs_table", T, U8)
+        xw_table = sbuf("xw_table", T, U32)
+        w2w = sbuf("w2w", N, U32)
+        w2s = sbuf("w2s", N, U8)
+        gate_sb = sbuf("gate_sb", S, F32)
+        windows = [sbuf(f"window{m}", U, F32) for m in range(N // P)]
 
         raw = {}
 
-        def load_weight_half(name, w, c):
-            cols = PIECES[name][c]
-            raw[name, c] = keep.tile(
-                [P, PACK, cols.stop - cols.start], F32, name=f"raw_{name}_{c}", tag=f"raw_{name}_{c}", align_bytes=64
-            )
-            nc.sync.dma_start(out=raw[name, c][:], in_=w.rearrange("(p j) c -> p j c", j=PACK)[:, :, cols])
+        def load_rows(name, w, u):
+            raw[name, u] = sbuf(f"raw_{name}_{u}", PAIR * H, F32)
+            nc.sync.dma_start(out=raw[name, u][:], in_=w.rearrange("(p u j) c -> p u (j c)", u=PAIR, j=PAIR)[:, u, :])
 
-        nc.vector.memset(xs_table[:].bitcast(I32), 0)
+        nc.gpsimd.memset(xs_table[:].bitcast(I32), 0)
+        nc.gpsimd.memset(w2s[:].bitcast(I32), 0)
         nc.sync.dma_start(offs_sb[:], offs)
-        load_weight_half("w1", w1, 0)
+        load_rows("w1", w1, 0)
         load_scale_rows(nc.sync, xs_table, x_scales[0])
-        load_weight_half("w1", w1, 1)
+        load_rows("w1", w1, 1)
         nc.sync.dma_start(out=xw_table[:].bitcast(I32), in_=x_words[0].rearrange("p c r -> p (c r)").bitcast(I32))
-        load_weight_half("w3", w3, 0)
-        load_weight_half("w3", w3, 1)
+        load_rows("w3", w3, 0)
+        load_rows("w3", w3, 1)
+        load_scale_rows(nc.sync, w2s, w2_scales[0])
+        nc.sync.dma_start(out=w2w[:].bitcast(I32), in_=w2_words[0].rearrange("p c r -> p (c r)").bitcast(I32))
+        nc.sync.dma_start(out=gate_sb[:], in_=gate)
         nc.sync.dma_start(dst_sb[:], dst)
 
         for half in (slice(0, U // 2), slice(U // 2, U)):
-            nc.vector.memset(windows[0][:, half], 0.0)
+            nc.gpsimd.memset(windows[0][:, half], 0.0)
             nc.scalar.activation(windows[1][:, half], windows[0][:, half], SILU)
 
         xw, xs = {}, {}
 
         def gather(into, table, dtype, first, count, tag):
-            picked = keep.tile([P, count], dtype, name=tag + "_picked", tag=tag, align_bytes=64)
+            picked = sbuf(f"picked_{tag}", count, dtype, tag)
             cols = slice(first // PER_COL, (first + count) // PER_COL)
             nc.vector.tensor_copy(picked[:], table[:].indirect(offs_sb[:, cols]))
             for c in range(count // CHUNK):
                 into[first // CHUNK + c] = picked[:, c * CHUNK : (c + 1) * CHUNK]
 
-        gather(xs, xs_table, U8, 0, S, "xs")
-
         codes, scales, grouped = {}, {}, {}
         for name in ("w1", "w3"):
-            grouped[name] = keep.tile([P, H * PACK], BF16, name=f"grouped_{name}", tag=f"grouped_{name}", align_bytes=64)
-            codes[name] = keep.tile([P, H], U32, name=f"codes_{name}", align_bytes=64)
-            scales[name] = keep.tile([P, H], U8, name=f"scales_{name}", align_bytes=64)
+            for s in range(PAIR):
+                grouped[name, s] = sbuf(f"grouped_{name}_{s}", PAIR * P * PACK, BF16)
+                codes[name, s] = sbuf(f"codes_{name}_{s}", PAIR * P, U32)
+                scales[name, s] = sbuf(f"scales_{name}_{s}", PAIR * P, U8)
 
-        def deal(copy, name, c, tiles):
-            dealt = grouped[name][:].rearrange("p (t m j) -> p m j t", t=PACK, j=PACK)
-            source = raw[name, c][:].rearrange("p j (m t) -> p m j t", t=PACK)
-            cols = PIECES[name][c]
-            copy(dealt[:, cols.start // PACK : cols.stop // PACK, :, tiles], source[:, :, :, tiles])
+        def deal(copy, name, u, s):
+            dealt = grouped[name, s][:].rearrange("p (t m j) -> p m j t", t=PAIR, j=PACK)
+            source = raw[name, u][:].rearrange("p (j m t) -> p m j t", j=PAIR, t=PACK)
+            copy(dealt[:, :, PAIR * u : PAIR * (u + 1), :], source[:, :, :, PAIR * s : PAIR * (s + 1)])
 
-        def quantise(name, tiles):
-            cols = slice(tiles.start * P, tiles.stop * P)
+        def quantise(name, s):
             nc.vector.quantize_mx(
-                out=codes[name][:, cols].bitcast(FP8X4),
-                scales=scales[name][:, cols],
-                in_=grouped[name][:, cols.start * PACK : cols.stop * PACK],
+                out=codes[name, s][:].bitcast(FP8X4), scales=scales[name, s][:], in_=grouped[name, s][:]
             )
 
-        all_tiles = slice(0, PACK)
-        tile_pairs = (slice(0, 2), slice(2, PACK))
-        deal(nc.scalar.copy, "w1", 0, all_tiles)
-        deal(nc.scalar.copy, "w1", 1, all_tiles)
-        quantise("w1", all_tiles)
-        gather(xw, xw_table, U32, 0, LATE, "xw0")
-        gather(xw, xw_table, U32, LATE, S - 2 * LATE, "xw1")
-        deal(nc.scalar.copy, "w3", 0, all_tiles)
-        for tiles in tile_pairs:
-            deal(nc.vector.tensor_copy, "w3", 1, tiles)
-        for tiles in tile_pairs:
-            quantise("w3", tiles)
-        gather(xw, xw_table, U32, S - LATE, LATE, "grouped_w3")
+        gather(xs, xs_table, U8, 0, S, "xs")
+        deal(nc.scalar.copy, "w1", 0, 0)
+        deal(nc.scalar.copy, "w1", 0, 1)
+        deal(nc.scalar.copy, "w1", 1, 1)
+        deal(nc.vector.tensor_copy, "w1", 1, 0)
+        quantise("w1", 0)
+        quantise("w1", 1)
+        gather(xw, xw_table, U32, 0, GROUP, "xw0")
+        gather(xw, xw_table, U32, GROUP, 3 * GROUP, "xw1")
+        for s in range(PAIR):
+            deal(nc.scalar.copy, "w3", 0, s)
+        for s in range(PAIR):
+            deal(nc.vector.tensor_copy, "w3", 1, s)
+        quantise("w3", 0)
+        quantise("w3", 1)
 
-        gate_sb = keep.tile([P, S], F32, name="gate_sb", tag="raw_w1_1", align_bytes=64)
-        nc.sync.dma_start(out=gate_sb[:], in_=gate)
-        w2w = keep.tile([P, N], U32, name="w2w", tag="raw_w1_0", align_bytes=64)
-        nc.sync.dma_start(out=w2w[:].bitcast(I32), in_=w2_words[0].rearrange("p c r -> p (c r)").bitcast(I32))
-        w2s = keep.tile([P, N], U8, name="w2s", tag="scale_rows", align_bytes=64)
-        nc.vector.memset(w2s[:].bitcast(I32), 0)
-        load_scale_rows(nc.sync, w2s, w2_scales[0])
-
-        def first_product(bank, name, c):
+        def first_product(name, c, bank):
+            acc = psum.tile([P, PACK, CHUNK], F32, name=f"acc_{name}_{c}", tag=f"bank{bank}")
             for t in range(PACK):
-                cols = slice(t * P, (t + 1) * P)
+                s, i = divmod(t, PAIR)
+                cols = slice(i * P, (i + 1) * P)
                 nc.tensor.matmul_mx(
-                    out=bank[:, t, :],
-                    lhsT=codes[name][:, cols].bitcast(FP8X4),
-                    lhsT_scale=scales[name][:, cols],
+                    out=acc[:, t, :],
+                    lhsT=codes[name, s][:, cols].bitcast(FP8X4),
+                    lhsT_scale=scales[name, s][:, cols],
                     rhs=xw[c].bitcast(FP8X4),
                     rhs_scale=xs[c],
                     start=True,
                     stop=True,
                 )
+            return acc[:].rearrange("p t n -> p n t")
 
-        n_chunks = S // CHUNK
-        per_half = HALF // CHUNK
-        silu_tiles = [
-            keep.tile([P, per_half, CHUNK, PACK], F32, name=f"silu{g}", tag=tag, align_bytes=64)
-            for g, tag in enumerate(("raw_w3_0", "silu1"))
-        ]
-        silu = [silu_tiles[c // per_half][:, c % per_half] for c in range(n_chunks)]
+        wide = CHUNK * PACK
+        silu_early = sbuf("silu_early", 4 * wide, F32, "raw_w3_0")
+        silu = [silu_early[:, : 2 * wide], silu_early[:, 2 * wide :]]
+        silu += [sbuf(f"silu{g}", 2 * wide, F32)[:] for g in (2, 3)]
+        linear = {g: sbuf(f"linear{g}", 2 * wide, F32) for g in (2, 3)}
 
-        def activate(c):
-            bank_a = psum.tile([P, PACK, CHUNK], F32, name="bank_a", tag=f"bank{c}")
-            first_product(bank_a, "w1", c)
-            nc.scalar.activation(silu[c], bank_a[:].rearrange("p t n -> p n t"), SILU)
+        def part(tile, i):
+            return tile[:, i * wide : (i + 1) * wide].rearrange("p (n t) -> p n t", t=PACK)
 
-        h = [keep.tile([P, HALF * PACK], BF16, name=f"h{g}", align_bytes=64) for g in range(S // HALF)]
-        y = {}
+        def activate(c, bank):
+            nc.scalar.activation(part(silu[c // 2], c % 2), first_product("w1", c, bank), SILU)
 
-        def multiply(c):
-            bank_b = psum.tile([P, PACK, CHUNK], F32, name="bank_b", tag=f"bank{(c + AHEAD) % n_chunks}")
-            first_product(bank_b, "w3", c)
-            g, i = divmod(c, per_half)
-            part = h[g][:, i * CHUNK * PACK : (i + 1) * CHUNK * PACK].rearrange("p (n t) -> p n t", t=PACK)
-            nc.vector.tensor_tensor(part, bank_b[:].rearrange("p t n -> p n t"), silu[c], MULT)
+        def multiply(h, c, bank):
+            nc.vector.tensor_tensor(part(h, c % 2), first_product("w3", c, bank), part(silu[c // 2], c % 2), MULT)
 
-        def second_product(g):
-            hw = keep.tile([P, HALF], U32, name=f"hw{g}", align_bytes=64)
-            hs = keep.tile([P, HALF], U8, name=f"hs{g}", align_bytes=64)
-            nc.vector.quantize_mx(out=hw[:].bitcast(FP8X4), scales=hs[:], in_=h[g][:])
-            for m in range(N // P):
-                cols = slice(m * P, (m + 1) * P)
-                bank_y = psum.tile([P, HALF], F32, name="bank_y", tag=f"bank{(AHEAD + 2 * g + m) % n_chunks}")
-                nc.tensor.matmul_mx(
-                    out=bank_y[:],
-                    lhsT=w2w[:, cols].bitcast(FP8X4),
-                    lhsT_scale=w2s[:, cols],
-                    rhs=hw[:].bitcast(FP8X4),
-                    rhs_scale=hs[:],
-                    start=True,
-                    stop=True,
-                )
-                y[g, m] = keep.tile([P, HALF], F32, name=f"y{g}_{m}", align_bytes=64)
-                nc.scalar.copy(y[g, m][:], bank_y[:])
+        def copy_linear(c, bank):
+            nc.scalar.copy(part(linear[c // 2], c % 2), first_product("w3", c, bank))
 
-        def scatter(g, m):
-            cols = slice(g * HALF // PER_COL, (g + 1) * HALF // PER_COL)
-            nc.vector.tensor_tensor(
-                windows[m][:].indirect(dst_sb[:, cols]), y[g, m][:], gate_sb[:, g * HALF : (g + 1) * HALF], MULT
+        def quantise_h(name, h, tokens):
+            hw = sbuf(f"hw{name}", tokens, U32)
+            hs = sbuf(f"hs{name}", tokens, U8)
+            nc.vector.quantize_mx(out=hw[:].bitcast(FP8X4), scales=hs[:], in_=h[:])
+            return hw, hs
+
+        def second_product(acc, m, hw, hs):
+            cols = slice(m * P, (m + 1) * P)
+            nc.tensor.matmul_mx(
+                out=acc,
+                lhsT=w2w[:, cols].bitcast(FP8X4),
+                lhsT_scale=w2s[:, cols],
+                rhs=hw[:].bitcast(FP8X4),
+                rhs_scale=hs[:],
+                start=True,
+                stop=True,
             )
 
-        for c in range(AHEAD):
-            activate(c)
-        for c in range(n_chunks):
-            multiply(c)
-            if c + AHEAD < n_chunks:
-                activate(c + AHEAD)
-            if c == per_half:
-                second_product(0)
-        scatter(0, 0)
-        second_product(1)
-        scatter(0, 1)
-        for m in range(N // P):
-            scatter(1, m)
+        def places(m, first, count):
+            return windows[m][:].indirect(dst_sb[:, first // PER_COL : (first + count) // PER_COL])
+
+        def weigh(acc, g, m):
+            y = sbuf(f"gated{g}_{m}", GROUP, F32)
+            nc.vector.tensor_tensor(y[:], acc, gate_sb[:, g * GROUP : (g + 1) * GROUP], MULT)
+            return y
+
+        h0 = sbuf("h0", 2 * wide, BF16)
+        h1 = sbuf("h1", 2 * wide, BF16, "h_late")
+        for c in range(4):
+            activate(c, c)
+        multiply(h0, 0, 4)
+        multiply(h0, 1, 5)
+        multiply(h1, 2, 6)
+        hw0, hs0 = quantise_h("0", h0, GROUP)
+        multiply(h1, 3, 7)
+        activate(4, 4)
+        activate(5, 5)
+        y0 = psum.tile([P, 2, GROUP], F32, name="y0", tag="bank6")
+        for m in range(2):
+            second_product(y0[:, m, :], m, hw0, hs0)
+        gated0 = [weigh(y0[:, m, :], 0, m) for m in range(2)]
+        hw1, hs1 = quantise_h("1", h1, GROUP)
+        copy_linear(4, 0)
+        copy_linear(5, 1)
+        y1 = psum.tile([P, 2, GROUP], F32, name="y1", tag="bank7")
+        for m in range(2):
+            second_product(y1[:, m, :], m, hw1, hs1)
+        activate(6, 2)
+        activate(7, 3)
+        copy_linear(6, 0)
+        copy_linear(7, 1)
+
+        h23 = sbuf("h23", 4 * wide, BF16, "h_late")
+        for g in (2, 3):
+            nc.gpsimd.tensor_tensor(h23[:, (g - 2) * 2 * wide : (g - 1) * 2 * wide], linear[g][:], silu[g], MULT)
+
+        for m in range(2):
+            nc.vector.tensor_copy(places(m, 0, GROUP), gated0[m][:])
+        gated10 = weigh(y1[:, 0, :], 1, 0)
+        nc.vector.tensor_copy(places(0, GROUP, GROUP), gated10[:])
+
+        hw23, hs23 = quantise_h("23", h23, 2 * GROUP)
+        y11 = sbuf("y11", GROUP, F32, "linear3")
+        nc.scalar.copy(y11[:], y1[:, 1, :])
+        nc.vector.tensor_tensor(places(1, GROUP, GROUP), y11[:], gate_sb[:, GROUP : 2 * GROUP], MULT)
+        for m in range(2):
+            acc = psum.tile([P, 2 * GROUP], F32, name=f"y23_{m}", tag=f"bank{2 + m}")
+            second_product(acc[:], m, hw23, hs23)
+            y = sbuf(f"y23_{m}", 2 * GROUP, F32)
+            nc.scalar.copy(y[:], acc[:])
+            nc.vector.tensor_tensor(places(m, 2 * GROUP, 2 * GROUP), y[:], gate_sb[:, 2 * GROUP :], MULT)
             nc.sync.dma_start(out=out[m * P : (m + 1) * P, :], in_=windows[m][:])

@@ -17,10 +17,11 @@ SILU = mybir.ActivationFunctionType.Silu
 
 P = 128
 PACK = 4
-PAIR = 2
 CHUNK = 128
 GROUP = 256
+PIECES = {"w1": (slice(0, H // 4), slice(H // 4, H)), "w3": (slice(0, H // 2), slice(H // 2, H))}
 PER_COL = 16
+LATE = 256
 
 
 def load_scale_rows(queue, plane, rows):
@@ -41,88 +42,93 @@ def tile_picked_route2_glusilu_p_kernel(
 
         offs_sb = keep.tile([P, S // PER_COL], U16, name="offs_sb")
         dst_sb = keep.tile([P, S // PER_COL], U16, name="dst_sb")
-        xs_table = sbuf("xs_table", T, U8)
-        xw_table = sbuf("xw_table", T, U32)
-        w2w = sbuf("w2w", N, U32)
-        w2s = sbuf("w2s", N, U8)
-        gate_sb = sbuf("gate_sb", S, F32)
-        windows = [sbuf(f"window{m}", U, F32) for m in range(N // P)]
+        xs_table = keep.tile([P, T], U8, name="xs_table", align_bytes=64)
+        xw_table = keep.tile([P, T], U32, name="xw_table", align_bytes=64)
+        windows = [keep.tile([P, U], F32, name=f"window{m}", align_bytes=64) for m in range(N // P)]
 
         raw = {}
 
-        def load_rows(name, w, u):
-            raw[name, u] = sbuf(f"raw_{name}_{u}", PAIR * H, F32)
-            nc.sync.dma_start(out=raw[name, u][:], in_=w.rearrange("(p u j) c -> p u (j c)", u=PAIR, j=PAIR)[:, u, :])
+        def load_weight_half(name, w, c):
+            cols = PIECES[name][c]
+            raw[name, c] = keep.tile(
+                [P, PACK, cols.stop - cols.start], F32, name=f"raw_{name}_{c}", tag=f"raw_{name}_{c}", align_bytes=64
+            )
+            nc.sync.dma_start(out=raw[name, c][:], in_=w.rearrange("(p j) c -> p j c", j=PACK)[:, :, cols])
 
-        nc.gpsimd.memset(xs_table[:].bitcast(I32), 0)
-        nc.gpsimd.memset(w2s[:].bitcast(I32), 0)
+        gate_sb = sbuf("gate_sb", S, F32)
+        w2w = sbuf("w2w", N, U32)
+        w2s = sbuf("w2s", N, U8)
+        nc.vector.memset(xs_table[:].bitcast(I32), 0)
+        nc.vector.memset(w2s[:].bitcast(I32), 0)
         nc.sync.dma_start(offs_sb[:], offs)
-        load_rows("w1", w1, 0)
+        load_weight_half("w1", w1, 0)
         load_scale_rows(nc.sync, xs_table, x_scales[0])
-        load_rows("w1", w1, 1)
+        load_weight_half("w1", w1, 1)
         nc.sync.dma_start(out=xw_table[:].bitcast(I32), in_=x_words[0].rearrange("p c r -> p (c r)").bitcast(I32))
-        load_rows("w3", w3, 0)
-        load_rows("w3", w3, 1)
+        load_weight_half("w3", w3, 0)
+        load_weight_half("w3", w3, 1)
         load_scale_rows(nc.sync, w2s, w2_scales[0])
         nc.sync.dma_start(out=w2w[:].bitcast(I32), in_=w2_words[0].rearrange("p c r -> p (c r)").bitcast(I32))
         nc.sync.dma_start(out=gate_sb[:], in_=gate)
         nc.sync.dma_start(dst_sb[:], dst)
 
         for half in (slice(0, U // 2), slice(U // 2, U)):
-            nc.gpsimd.memset(windows[0][:, half], 0.0)
+            nc.vector.memset(windows[0][:, half], 0.0)
             nc.scalar.activation(windows[1][:, half], windows[0][:, half], SILU)
 
         xw, xs = {}, {}
 
         def gather(into, table, dtype, first, count, tag):
-            picked = sbuf(f"picked_{tag}", count, dtype, tag)
+            picked = keep.tile([P, count], dtype, name=tag + "_picked", tag=tag, align_bytes=64)
             cols = slice(first // PER_COL, (first + count) // PER_COL)
             nc.vector.tensor_copy(picked[:], table[:].indirect(offs_sb[:, cols]))
             for c in range(count // CHUNK):
                 into[first // CHUNK + c] = picked[:, c * CHUNK : (c + 1) * CHUNK]
 
+        gather(xs, xs_table, U8, 0, S, "xs")
+
         codes, scales, grouped = {}, {}, {}
         for name in ("w1", "w3"):
-            for s in range(PAIR):
-                grouped[name, s] = sbuf(f"grouped_{name}_{s}", PAIR * P * PACK, BF16)
-                codes[name, s] = sbuf(f"codes_{name}_{s}", PAIR * P, U32)
-                scales[name, s] = sbuf(f"scales_{name}_{s}", PAIR * P, U8)
+            grouped[name] = keep.tile([P, H * PACK], BF16, name=f"grouped_{name}", tag=f"grouped_{name}", align_bytes=64)
+            codes[name] = keep.tile([P, H], U32, name=f"codes_{name}", align_bytes=64)
+            scales[name] = keep.tile([P, H], U8, name=f"scales_{name}", align_bytes=64)
 
-        def deal(copy, name, u, s):
-            dealt = grouped[name, s][:].rearrange("p (t m j) -> p m j t", t=PAIR, j=PACK)
-            source = raw[name, u][:].rearrange("p (j m t) -> p m j t", j=PAIR, t=PACK)
-            copy(dealt[:, :, PAIR * u : PAIR * (u + 1), :], source[:, :, :, PAIR * s : PAIR * (s + 1)])
+        def deal(copy, name, c, tiles):
+            dealt = grouped[name][:].rearrange("p (t m j) -> p m j t", t=PACK, j=PACK)
+            source = raw[name, c][:].rearrange("p j (m t) -> p m j t", t=PACK)
+            cols = PIECES[name][c]
+            copy(dealt[:, cols.start // PACK : cols.stop // PACK, :, tiles], source[:, :, :, tiles])
 
-        def quantise(name, s):
+        def quantise(name, tiles):
+            cols = slice(tiles.start * P, tiles.stop * P)
             nc.vector.quantize_mx(
-                out=codes[name, s][:].bitcast(FP8X4), scales=scales[name, s][:], in_=grouped[name, s][:]
+                out=codes[name][:, cols].bitcast(FP8X4),
+                scales=scales[name][:, cols],
+                in_=grouped[name][:, cols.start * PACK : cols.stop * PACK],
             )
 
-        gather(xs, xs_table, U8, 0, S, "xs")
-        deal(nc.scalar.copy, "w1", 0, 0)
-        deal(nc.scalar.copy, "w1", 0, 1)
-        deal(nc.scalar.copy, "w1", 1, 1)
-        deal(nc.vector.tensor_copy, "w1", 1, 0)
-        quantise("w1", 0)
-        quantise("w1", 1)
-        gather(xw, xw_table, U32, 0, GROUP, "xw0")
-        gather(xw, xw_table, U32, GROUP, 3 * GROUP, "xw1")
-        for s in range(PAIR):
-            deal(nc.scalar.copy, "w3", 0, s)
-        for s in range(PAIR):
-            deal(nc.vector.tensor_copy, "w3", 1, s)
-        quantise("w3", 0)
-        quantise("w3", 1)
+        all_tiles = slice(0, PACK)
+        tile_pairs = (slice(0, 2), slice(2, PACK))
+        deal(nc.scalar.copy, "w1", 0, all_tiles)
+        deal(nc.scalar.copy, "w1", 1, all_tiles)
+        quantise("w1", all_tiles)
+        gather(xw, xw_table, U32, 0, LATE, "xw0")
+        gather(xw, xw_table, U32, LATE, S - 2 * LATE, "xw1")
+        deal(nc.scalar.copy, "w3", 0, all_tiles)
+        for tiles in tile_pairs:
+            deal(nc.vector.tensor_copy, "w3", 1, tiles)
+        for tiles in tile_pairs:
+            quantise("w3", tiles)
+        gather(xw, xw_table, U32, S - LATE, LATE, "grouped_w3")
 
         def first_product(name, c, bank):
             acc = psum.tile([P, PACK, CHUNK], F32, name=f"acc_{name}_{c}", tag=f"bank{bank}")
             for t in range(PACK):
-                s, i = divmod(t, PAIR)
-                cols = slice(i * P, (i + 1) * P)
+                cols = slice(t * P, (t + 1) * P)
                 nc.tensor.matmul_mx(
                     out=acc[:, t, :],
-                    lhsT=codes[name, s][:, cols].bitcast(FP8X4),
-                    lhsT_scale=scales[name, s][:, cols],
+                    lhsT=codes[name][:, cols].bitcast(FP8X4),
+                    lhsT_scale=scales[name][:, cols],
                     rhs=xw[c].bitcast(FP8X4),
                     rhs_scale=xs[c],
                     start=True,

@@ -1,6 +1,7 @@
 from contextlib import ExitStack
 
 import concourse.mybir as mybir
+from concourse.masks import make_identity
 
 K, T, S, H, N, U = 512, 2048, 1024, 512, 256, 2048
 FLOPS = 2 * S * (2 * K * H + H * N)
@@ -13,6 +14,7 @@ U16 = mybir.dt.uint16
 U8 = mybir.dt.uint8
 FP8X4 = mybir.dt.float8_e4m3fn_x4
 MULT = mybir.AluOpType.mult
+COPY = mybir.ActivationFunctionType.Copy
 SILU = mybir.ActivationFunctionType.Silu
 
 P = 128
@@ -55,13 +57,16 @@ def tile_picked_route2_glusilu_p_kernel(
             )
             nc.sync.dma_start(out=raw[name, c][:], in_=w.rearrange("(p j) c -> p j c", j=PACK)[:, :, cols])
 
-        gate_sb = sbuf("gate_sb", S, F32)
+        gate_first = sbuf("gate_first", GROUP, F32)
+        gate_rest = sbuf("gate_rest", S - GROUP, F32)
+        gate_col = sbuf("gate_col", GROUP // CHUNK, F32)
+        identity = sbuf("identity", P, F32)
         w2w = sbuf("w2w", N, U32)
         w2s = sbuf("w2s", N, U8)
         nc.vector.memset(xs_table[:].bitcast(I32), 0)
         nc.vector.memset(w2s[:].bitcast(I32), 0)
-        nc.sync.dma_start(offs_sb[:], offs)
         load_weight_half("w1", w1, 0)
+        nc.sync.dma_start(offs_sb[:], offs)
         load_scale_rows(nc.sync, xs_table, x_scales[0])
         load_weight_half("w1", w1, 1)
         nc.sync.dma_start(out=xw_table[:].bitcast(I32), in_=x_words[0].rearrange("p c r -> p (c r)").bitcast(I32))
@@ -69,8 +74,13 @@ def tile_picked_route2_glusilu_p_kernel(
         load_weight_half("w3", w3, 1)
         load_scale_rows(nc.sync, w2s, w2_scales[0])
         nc.sync.dma_start(out=w2w[:].bitcast(I32), in_=w2_words[0].rearrange("p c r -> p (c r)").bitcast(I32))
-        nc.sync.dma_start(out=gate_sb[:], in_=gate)
+        nc.sync.dma_start(out=gate_first[:], in_=gate[:, :GROUP])
         nc.sync.dma_start(dst_sb[:], dst)
+        with nc.allow_non_contiguous_dma(reason="one gate value a partition"):
+            nc.sync.dma_start(out=gate_col[:], in_=gate[0, GROUP : 2 * GROUP].rearrange("(c p) -> p c", p=P))
+        nc.sync.dma_start(out=gate_rest[:], in_=gate[:, GROUP:])
+        nc.vector.memset(identity[:], 0.0)
+        make_identity(nc, identity[:], nomemset=True)
 
         for half in (slice(0, U // 2), slice(U // 2, U)):
             nc.vector.memset(windows[0][:, half], 0.0)
@@ -158,7 +168,7 @@ def tile_picked_route2_glusilu_p_kernel(
             hw = sbuf(f"hw{name}", tokens, U32)
             hs = sbuf(f"hs{name}", tokens, U8)
             nc.vector.quantize_mx(out=hw[:].bitcast(FP8X4), scales=hs[:], in_=h[:])
-            return hw, hs
+            return hw[:], hs[:]
 
         def second_product(acc, m, hw, hs):
             cols = slice(m * P, (m + 1) * P)
@@ -166,8 +176,8 @@ def tile_picked_route2_glusilu_p_kernel(
                 out=acc,
                 lhsT=w2w[:, cols].bitcast(FP8X4),
                 lhsT_scale=w2s[:, cols],
-                rhs=hw[:].bitcast(FP8X4),
-                rhs_scale=hs[:],
+                rhs=hw.bitcast(FP8X4),
+                rhs_scale=hs,
                 start=True,
                 stop=True,
             )
@@ -175,9 +185,32 @@ def tile_picked_route2_glusilu_p_kernel(
         def places(m, first, count):
             return windows[m][:].indirect(dst_sb[:, first // PER_COL : (first + count) // PER_COL])
 
-        def weigh(acc, g, m):
+        def turned_product(acc, g, m, hw, hs):
+            cols = slice(m * P, (m + 1) * P)
+            rows = sbuf(f"rows{g}_{m}", GROUP, F32)
+            for i in range(GROUP // CHUNK):
+                tokens = slice(i * CHUNK, (i + 1) * CHUNK)
+                nc.tensor.matmul_mx(
+                    out=acc[:, tokens],
+                    lhsT=hw[:, tokens].bitcast(FP8X4),
+                    lhsT_scale=hs[:, tokens],
+                    rhs=w2w[:, cols].bitcast(FP8X4),
+                    rhs_scale=w2s[:, cols],
+                    start=True,
+                    stop=True,
+                )
+            for i in range(GROUP // CHUNK):
+                tokens = slice(i * CHUNK, (i + 1) * CHUNK)
+                nc.scalar.activation(rows[:, tokens], acc[:, tokens], COPY, scale=gate_col[:, i : i + 1])
+            return rows
+
+        def turn_back(rows, g, m, bank):
+            acc = psum.tile([P, GROUP], F32, name=f"back{g}_{m}", tag=f"bank{bank}")
+            for i in range(GROUP // CHUNK):
+                tokens = slice(i * CHUNK, (i + 1) * CHUNK)
+                nc.tensor.transpose(acc[:, tokens], rows[:, tokens], identity[:])
             y = sbuf(f"gated{g}_{m}", GROUP, F32)
-            nc.vector.tensor_tensor(y[:], acc, gate_sb[:, g * GROUP : (g + 1) * GROUP], MULT)
+            nc.scalar.copy(y[:], acc[:])
             return y
 
         h0 = sbuf("h0", 2 * wide, BF16)
@@ -186,43 +219,49 @@ def tile_picked_route2_glusilu_p_kernel(
             activate(c, c)
         multiply(h0, 0, 4)
         multiply(h0, 1, 5)
+        activate(4, 3)
+        copy_linear(4, 0)
         multiply(h1, 2, 6)
+        activate(5, 4)
+        copy_linear(5, 1)
         hw0, hs0 = quantise_h("0", h0, GROUP)
         multiply(h1, 3, 7)
-        activate(4, 4)
-        activate(5, 5)
         y0 = psum.tile([P, 2, GROUP], F32, name="y0", tag="bank6")
+        gated0 = []
         for m in range(2):
             second_product(y0[:, m, :], m, hw0, hs0)
-        gated0 = [weigh(y0[:, m, :], 0, m) for m in range(2)]
-        hw1, hs1 = quantise_h("1", h1, GROUP)
-        copy_linear(4, 0)
-        copy_linear(5, 1)
-        y1 = psum.tile([P, 2, GROUP], F32, name="y1", tag="bank7")
         for m in range(2):
-            second_product(y1[:, m, :], m, hw1, hs1)
+            gated0.append(sbuf(f"gated0_{m}", GROUP, F32))
+            nc.vector.tensor_tensor(gated0[m][:], y0[:, m, :], gate_first[:], MULT)
+        hw1, hs1 = quantise_h("1", h1, GROUP)
         activate(6, 2)
-        activate(7, 3)
+        activate(7, 5)
         copy_linear(6, 0)
+        y10 = psum.tile([P, GROUP], F32, name="y10", tag="bank7")
+        rows10 = turned_product(y10, 1, 0, hw1, hs1)
+        gated10 = turn_back(rows10, 1, 0, 3)
         copy_linear(7, 1)
 
         h23 = sbuf("h23", 4 * wide, BF16, "h_late")
         for g in (2, 3):
             nc.gpsimd.tensor_tensor(h23[:, (g - 2) * 2 * wide : (g - 1) * 2 * wide], linear[g][:], silu[g], MULT)
 
-        for m in range(2):
-            nc.vector.tensor_copy(places(m, 0, GROUP), gated0[m][:])
-        gated10 = weigh(y1[:, 0, :], 1, 0)
+        nc.vector.tensor_copy(places(0, 0, GROUP), gated0[0][:])
+        nc.vector.tensor_copy(places(1, 0, GROUP), gated0[1][:])
         nc.vector.tensor_copy(places(0, GROUP, GROUP), gated10[:])
 
         hw23, hs23 = quantise_h("23", h23, 2 * GROUP)
+        acc11 = psum.tile([P, GROUP], F32, name="acc11", tag="bank3")
+        second_product(acc11[:], 1, hw1, hs1)
         y11 = sbuf("y11", GROUP, F32, "linear3")
-        nc.scalar.copy(y11[:], y1[:, 1, :])
-        nc.vector.tensor_tensor(places(1, GROUP, GROUP), y11[:], gate_sb[:, GROUP : 2 * GROUP], MULT)
+        nc.scalar.copy(y11[:], acc11[:])
+        nc.vector.tensor_tensor(places(1, GROUP, GROUP), y11[:], gate_rest[:, :GROUP], MULT)
         for m in range(2):
-            acc = psum.tile([P, 2 * GROUP], F32, name=f"y23_{m}", tag=f"bank{2 + m}")
-            second_product(acc[:], m, hw23, hs23)
             y = sbuf(f"y23_{m}", 2 * GROUP, F32)
-            nc.scalar.copy(y[:], acc[:])
-            nc.vector.tensor_tensor(places(m, 2 * GROUP, 2 * GROUP), y[:], gate_sb[:, 2 * GROUP :], MULT)
+            for i in range(2):
+                tokens = slice(i * GROUP, (i + 1) * GROUP)
+                acc = psum.tile([P, GROUP], F32, name=f"acc23_{m}_{i}", tag=f"bank{2 * m + i}")
+                second_product(acc[:], m, hw23[:, tokens], hs23[:, tokens])
+                nc.scalar.copy(y[:, tokens], acc[:])
+            nc.vector.tensor_tensor(places(m, 2 * GROUP, 2 * GROUP), y[:], gate_rest[:, GROUP:], MULT)
             nc.sync.dma_start(out=out[m * P : (m + 1) * P, :], in_=windows[m][:])

@@ -14,6 +14,7 @@ U16 = mybir.dt.uint16
 U8 = mybir.dt.uint8
 FP8X4 = mybir.dt.float8_e4m3fn_x4
 MULT = mybir.AluOpType.mult
+ADD = mybir.AluOpType.add
 COPY = mybir.ActivationFunctionType.Copy
 SILU = mybir.ActivationFunctionType.Silu
 
@@ -26,9 +27,9 @@ PER_COL = 16
 LATE = 256
 
 
-def load_scale_rows(queue, plane, rows):
+def load_scale_rows(queues, plane, rows):
     for q in range(4):
-        queue.dma_start(out=plane[32 * q : 32 * q + 4, :].bitcast(I32), in_=rows[4 * q : 4 * q + 4, :].bitcast(I32))
+        queues[q % len(queues)].dma_start(out=plane[32 * q : 32 * q + 4, :].bitcast(I32), in_=rows[4 * q : 4 * q + 4, :].bitcast(I32))
 
 
 def tile_picked_route2_glusilu_p_kernel(
@@ -67,12 +68,12 @@ def tile_picked_route2_glusilu_p_kernel(
         nc.vector.memset(w2s[:].bitcast(I32), 0)
         load_weight_half("w1", w1, 0)
         nc.sync.dma_start(offs_sb[:], offs)
-        load_scale_rows(nc.sync, xs_table, x_scales[0])
+        load_scale_rows((nc.sync, nc.scalar), xs_table, x_scales[0])
         load_weight_half("w1", w1, 1)
         nc.sync.dma_start(out=xw_table[:].bitcast(I32), in_=x_words[0].rearrange("p c r -> p (c r)").bitcast(I32))
         load_weight_half("w3", w3, 0)
         load_weight_half("w3", w3, 1)
-        load_scale_rows(nc.sync, w2s, w2_scales[0])
+        load_scale_rows((nc.sync,), w2s, w2_scales[0])
         nc.sync.dma_start(out=w2w[:].bitcast(I32), in_=w2_words[0].rearrange("p c r -> p (c r)").bitcast(I32))
         nc.sync.dma_start(out=gate_first[:], in_=gate[:, :GROUP])
         nc.sync.dma_start(dst_sb[:], dst)
@@ -82,9 +83,11 @@ def tile_picked_route2_glusilu_p_kernel(
         nc.vector.memset(identity[:], 0.0)
         make_identity(nc, identity[:], nomemset=True)
 
-        for half in (slice(0, U // 2), slice(U // 2, U)):
+        halves = (slice(0, U // 2), slice(U // 2, U))
+        for half in halves:
             nc.vector.memset(windows[0][:, half], 0.0)
-            nc.scalar.activation(windows[1][:, half], windows[0][:, half], SILU)
+        nc.scalar.activation(windows[1][:, halves[0]], windows[0][:, halves[0]], SILU)
+        nc.gpsimd.tensor_scalar(windows[1][:, halves[1]], windows[0][:, halves[1]], 1.0, 0.0, MULT, ADD)
 
         xw, xs = {}, {}
 
@@ -129,7 +132,7 @@ def tile_picked_route2_glusilu_p_kernel(
             deal(nc.vector.tensor_copy, "w3", 1, tiles)
         for tiles in tile_pairs:
             quantise("w3", tiles)
-        gather(xw, xw_table, U32, S - LATE, LATE, "grouped_w3")
+        gather(xw, xw_table, U32, S - LATE, LATE, "raw_w3_1")
 
         def first_product(name, c, bank):
             acc = psum.tile([P, PACK, CHUNK], F32, name=f"acc_{name}_{c}", tag=f"bank{bank}")

@@ -29,7 +29,7 @@ LATE = 256
 
 def load_scale_rows(queues, plane, rows):
     for q in range(4):
-        queues[q % len(queues)].dma_start(out=plane[32 * q : 32 * q + 4, :].bitcast(I32), in_=rows[4 * q : 4 * q + 4, :].bitcast(I32))
+        queues[q * len(queues) // 4].dma_start(out=plane[32 * q : 32 * q + 4, :].bitcast(I32), in_=rows[4 * q : 4 * q + 4, :].bitcast(I32))
 
 
 def tile_picked_route2_glusilu_p_kernel(
@@ -267,4 +267,5 @@ def tile_picked_route2_glusilu_p_kernel(
                 second_product(acc[:], m, hw23[:, tokens], hs23[:, tokens])
                 nc.scalar.copy(y[:, tokens], acc[:])
             nc.vector.tensor_tensor(places(m, 2 * GROUP, 2 * GROUP), y[:], gate_rest[:, GROUP:], MULT)
-            nc.sync.dma_start(out=out[m * P : (m + 1) * P, :], in_=windows[m][:])
+            for queue, half in zip((nc.sync, nc.scalar), halves):
+                queue.dma_start(out=out[m * P : (m + 1) * P, half], in_=windows[m][:, half])

@@ -207,14 +207,12 @@ def tile_picked_route2_glusilu_p_kernel(
                 nc.scalar.activation(rows[:, tokens], acc[:, tokens], COPY, scale=gate_col[:, i : i + 1])
             return rows
 
-        def turn_back(rows, g, m, bank):
-            acc = psum.tile([P, GROUP], F32, name=f"back{g}_{m}", tag=f"bank{bank}")
+        def turn_back(rows, y, bank):
+            acc = psum.tile([P, GROUP], F32, name="back", tag=f"bank{bank}")
             for i in range(GROUP // CHUNK):
                 tokens = slice(i * CHUNK, (i + 1) * CHUNK)
                 nc.tensor.transpose(acc[:, tokens], rows[:, tokens], identity[:])
-            y = sbuf(f"gated{g}_{m}", GROUP, F32)
-            nc.scalar.copy(y[:], acc[:])
-            return y
+            nc.scalar.copy(y, acc[:])
 
         h0 = sbuf("h0", 2 * wide, BF16)
         h1 = sbuf("h1", 2 * wide, BF16, "h_late")
@@ -230,28 +228,27 @@ def tile_picked_route2_glusilu_p_kernel(
         hw0, hs0 = quantise_h("0", h0, GROUP)
         multiply(h1, 3, 7)
         y0 = psum.tile([P, 2, GROUP], F32, name="y0", tag="bank6")
-        gated0 = []
-        for m in range(2):
+        for m in (1, 0):
             second_product(y0[:, m, :], m, hw0, hs0)
-        for m in range(2):
-            gated0.append(sbuf(f"gated0_{m}", GROUP, F32))
-            nc.vector.tensor_tensor(gated0[m][:], y0[:, m, :], gate_first[:], MULT)
+        gated0 = sbuf("gated0", 2 * GROUP, F32)
+        gated1 = sbuf("gated1", GROUP, F32)
+        nc.vector.tensor_tensor(gated1[:], y0[:, 1, :], gate_first[:], MULT)
         hw1, hs1 = quantise_h("1", h1, GROUP)
+        nc.vector.tensor_tensor(gated0[:, :GROUP], y0[:, 0, :], gate_first[:], MULT)
         activate(6, 2)
-        activate(7, 5)
         copy_linear(6, 0)
         y10 = psum.tile([P, GROUP], F32, name="y10", tag="bank7")
         rows10 = turned_product(y10, 1, 0, hw1, hs1)
-        gated10 = turn_back(rows10, 1, 0, 3)
+        turn_back(rows10, gated0[:, GROUP:], 3)
+        activate(7, 7)
         copy_linear(7, 1)
 
         h23 = sbuf("h23", 4 * wide, BF16, "h_late")
         for g in (2, 3):
             nc.gpsimd.tensor_tensor(h23[:, (g - 2) * 2 * wide : (g - 1) * 2 * wide], linear[g][:], silu[g], MULT)
 
-        nc.vector.tensor_copy(places(0, 0, GROUP), gated0[0][:])
-        nc.vector.tensor_copy(places(1, 0, GROUP), gated0[1][:])
-        nc.vector.tensor_copy(places(0, GROUP, GROUP), gated10[:])
+        nc.vector.tensor_copy(places(1, 0, GROUP), gated1[:])
+        nc.vector.tensor_copy(places(0, 0, 2 * GROUP), gated0[:])
 
         hw23, hs23 = quantise_h("23", h23, 2 * GROUP)
         acc11 = psum.tile([P, GROUP], F32, name="acc11", tag="bank3")

@@ -112,6 +112,10 @@ def tile_picked_route2_glusilu_p_kernel(
             cols = PIECES[name][c]
             copy(dealt[:, cols.start // PACK : cols.stop // PACK, :, tiles], source[:, :, :, tiles])
 
+        def gpsimd_cast(target, source):
+            order = "p m j t -> p t m j"
+            nc.gpsimd.tensor_scalar(target.rearrange(order), source.rearrange(order), 1.0, 0.0, MULT, ADD)
+
         def quantise(name, tiles):
             cols = slice(tiles.start * P, tiles.stop * P)
             nc.vector.quantize_mx(
@@ -127,7 +131,8 @@ def tile_picked_route2_glusilu_p_kernel(
         quantise("w1", all_tiles)
         gather(xw, xw_table, U32, 0, LATE, "xw0")
         gather(xw, xw_table, U32, LATE, S - 2 * LATE, "xw1")
-        deal(nc.scalar.copy, "w3", 0, all_tiles)
+        deal(nc.scalar.copy, "w3", 0, tile_pairs[0])
+        deal(gpsimd_cast, "w3", 0, tile_pairs[1])
         for tiles in tile_pairs:
             deal(nc.vector.tensor_copy, "w3", 1, tiles)
         for tiles in tile_pairs:
@@ -220,9 +225,9 @@ def tile_picked_route2_glusilu_p_kernel(
             activate(c, c)
         multiply(h0, 0, 4)
         multiply(h0, 1, 5)
-        activate(4, 3)
-        copy_linear(4, 0)
         multiply(h1, 2, 6)
+        copy_linear(4, 0)
+        activate(4, 3)
         activate(5, 4)
         copy_linear(5, 1)
         hw0, hs0 = quantise_h("0", h0, GROUP)

@@ -22,7 +22,7 @@ P = 128
 PACK = 4
 CHUNK = 128
 GROUP = 256
-PIECES = {"w1": (slice(0, H // 4), slice(H // 4, H)), "w3": (slice(0, H // 2), slice(H // 2, H))}
+PIECES = {"w1": (slice(0, H // 4), slice(H // 4, H)), "w3": (slice(0, H // 4), slice(H // 4, H // 2), slice(H // 2, H))}
 PER_COL = 16
 LATE = 256
 
@@ -71,8 +71,8 @@ def tile_picked_route2_glusilu_p_kernel(
         load_scale_rows((nc.sync, nc.scalar), xs_table, x_scales[0])
         load_weight_half("w1", w1, 1)
         nc.sync.dma_start(out=xw_table[:].bitcast(I32), in_=x_words[0].rearrange("p c r -> p (c r)").bitcast(I32))
-        load_weight_half("w3", w3, 0)
-        load_weight_half("w3", w3, 1)
+        for c in range(3):
+            load_weight_half("w3", w3, c)
         load_scale_rows((nc.sync,), w2s, w2_scales[0])
         nc.sync.dma_start(out=w2w[:].bitcast(I32), in_=w2_words[0].rearrange("p c r -> p (c r)").bitcast(I32))
         nc.sync.dma_start(out=gate_first[:], in_=gate[:, :GROUP])
@@ -127,17 +127,18 @@ def tile_picked_route2_glusilu_p_kernel(
         all_tiles = slice(0, PACK)
         tile_pairs = (slice(0, 2), slice(2, PACK))
         deal(nc.scalar.copy, "w1", 0, all_tiles)
-        deal(nc.scalar.copy, "w1", 1, all_tiles)
-        quantise("w1", all_tiles)
+        for tiles in tile_pairs:
+            deal(nc.scalar.copy, "w1", 1, tiles)
+            quantise("w1", tiles)
         gather(xw, xw_table, U32, 0, LATE, "xw0")
         gather(xw, xw_table, U32, LATE, S - 2 * LATE, "xw1")
-        deal(nc.scalar.copy, "w3", 0, tile_pairs[0])
-        deal(gpsimd_cast, "w3", 0, tile_pairs[1])
+        deal(nc.scalar.copy, "w3", 0, all_tiles)
+        deal(gpsimd_cast, "w3", 1, all_tiles)
         for tiles in tile_pairs:
-            deal(nc.vector.tensor_copy, "w3", 1, tiles)
+            deal(nc.vector.tensor_copy, "w3", 2, tiles)
         for tiles in tile_pairs:
             quantise("w3", tiles)
-        gather(xw, xw_table, U32, S - LATE, LATE, "raw_w3_1")
+        gather(xw, xw_table, U32, S - LATE, LATE, "raw_w3_2")
 
         def first_product(name, c, bank):
             acc = psum.tile([P, PACK, CHUNK], F32, name=f"acc_{name}_{c}", tag=f"bank{bank}")
@@ -226,10 +227,10 @@ def tile_picked_route2_glusilu_p_kernel(
         multiply(h0, 0, 4)
         multiply(h0, 1, 5)
         multiply(h1, 2, 6)
-        copy_linear(4, 0)
-        activate(4, 3)
-        activate(5, 4)
-        copy_linear(5, 1)
+        activate(4, 0)
+        copy_linear(4, 1)
+        activate(5, 3)
+        copy_linear(5, 2)
         hw0, hs0 = quantise_h("0", h0, GROUP)
         multiply(h1, 3, 7)
         y0 = psum.tile([P, 2, GROUP], F32, name="y0", tag="bank6")
@@ -240,13 +241,15 @@ def tile_picked_route2_glusilu_p_kernel(
         nc.vector.tensor_tensor(gated1[:], y0[:, 1, :], gate_first[:], MULT)
         hw1, hs1 = quantise_h("1", h1, GROUP)
         nc.vector.tensor_tensor(gated0[:, :GROUP], y0[:, 0, :], gate_first[:], MULT)
-        activate(6, 2)
+        activate(6, 4)
         copy_linear(6, 0)
         y10 = psum.tile([P, GROUP], F32, name="y10", tag="bank7")
         rows10 = turned_product(y10, 1, 0, hw1, hs1)
         turn_back(rows10, gated0[:, GROUP:], 3)
-        activate(7, 7)
-        copy_linear(7, 1)
+        for name, func, tile, bank in (("w1", SILU, silu[3], 5), ("w3", COPY, linear[3], 1)):
+            product = first_product(name, 7, bank)
+            for tokens in (slice(0, CHUNK // 2), slice(CHUNK // 2, CHUNK)):
+                nc.scalar.activation(part(tile, 1)[:, tokens], product[:, tokens], func)
 
         h23 = sbuf("h23", 4 * wide, BF16, "h_late")
         for g in (2, 3):

@@ -22,7 +22,7 @@ P = 128
 PACK = 4
 CHUNK = 128
 GROUP = 256
-PIECES = {"w1": (slice(0, H // 4), slice(H // 4, H)), "w3": (slice(0, H // 4), slice(H // 4, H // 2), slice(H // 2, H))}
+PIECES = {"w1": (slice(0, H // 4), slice(H // 4, H)), "w3": (slice(0, H // 2), slice(H // 2, H))}
 PER_COL = 16
 LATE = 256
 
@@ -71,7 +71,7 @@ def tile_picked_route2_glusilu_p_kernel(
         load_scale_rows((nc.sync, nc.scalar), xs_table, x_scales[0])
         load_weight_half("w1", w1, 1)
         nc.sync.dma_start(out=xw_table[:].bitcast(I32), in_=x_words[0].rearrange("p c r -> p (c r)").bitcast(I32))
-        for c in range(3):
+        for c in range(2):
             load_weight_half("w3", w3, c)
         load_scale_rows((nc.sync,), w2s, w2_scales[0])
         nc.sync.dma_start(out=w2w[:].bitcast(I32), in_=w2_words[0].rearrange("p c r -> p (c r)").bitcast(I32))
@@ -132,13 +132,13 @@ def tile_picked_route2_glusilu_p_kernel(
             quantise("w1", tiles)
         gather(xw, xw_table, U32, 0, LATE, "xw0")
         gather(xw, xw_table, U32, LATE, S - 2 * LATE, "xw1")
-        deal(nc.scalar.copy, "w3", 0, all_tiles)
-        deal(gpsimd_cast, "w3", 1, all_tiles)
+        deal(nc.scalar.copy, "w3", 0, tile_pairs[0])
+        deal(gpsimd_cast, "w3", 0, tile_pairs[1])
         for tiles in tile_pairs:
-            deal(nc.vector.tensor_copy, "w3", 2, tiles)
+            deal(nc.vector.tensor_copy, "w3", 1, tiles)
         for tiles in tile_pairs:
             quantise("w3", tiles)
-        gather(xw, xw_table, U32, S - LATE, LATE, "raw_w3_2")
+        gather(xw, xw_table, U32, S - LATE, LATE, "raw_w3_1")
 
         def first_product(name, c, bank):
             acc = psum.tile([P, PACK, CHUNK], F32, name=f"acc_{name}_{c}", tag=f"bank{bank}")
@@ -194,13 +194,14 @@ def tile_picked_route2_glusilu_p_kernel(
         def places(m, first, count):
             return windows[m][:].indirect(dst_sb[:, first // PER_COL : (first + count) // PER_COL])
 
-        def turned_product(acc, g, m, hw, hs):
+        def turned_unit(y, m, hw, hs, banks):
             cols = slice(m * P, (m + 1) * P)
-            rows = sbuf(f"rows{g}_{m}", GROUP, F32)
-            for i in range(GROUP // CHUNK):
-                tokens = slice(i * CHUNK, (i + 1) * CHUNK)
+            rows = sbuf("rows", GROUP, F32)
+            chunks = [slice(i * CHUNK, (i + 1) * CHUNK) for i in range(GROUP // CHUNK)]
+            for i, tokens in enumerate(chunks):
+                acc = psum.tile([P, CHUNK], F32, name=f"turned{i}", tag=f"bank{banks[i]}")
                 nc.tensor.matmul_mx(
-                    out=acc[:, tokens],
+                    out=acc[:],
                     lhsT=hw[:, tokens].bitcast(FP8X4),
                     lhsT_scale=hs[:, tokens],
                     rhs=w2w[:, cols].bitcast(FP8X4),
@@ -208,17 +209,11 @@ def tile_picked_route2_glusilu_p_kernel(
                     start=True,
                     stop=True,
                 )
-            for i in range(GROUP // CHUNK):
-                tokens = slice(i * CHUNK, (i + 1) * CHUNK)
-                nc.scalar.activation(rows[:, tokens], acc[:, tokens], COPY, scale=gate_col[:, i : i + 1])
-            return rows
-
-        def turn_back(rows, y, bank):
-            acc = psum.tile([P, GROUP], F32, name="back", tag=f"bank{bank}")
-            for i in range(GROUP // CHUNK):
-                tokens = slice(i * CHUNK, (i + 1) * CHUNK)
-                nc.tensor.transpose(acc[:, tokens], rows[:, tokens], identity[:])
-            nc.scalar.copy(y, acc[:])
+                nc.scalar.activation(rows[:, tokens], acc[:], COPY, scale=gate_col[:, i : i + 1])
+            for i, tokens in enumerate(chunks):
+                acc = psum.tile([P, CHUNK], F32, name=f"back{i}", tag=f"bank{banks[2 + i]}")
+                nc.tensor.transpose(acc[:], rows[:, tokens], identity[:])
+                nc.scalar.copy(y[:, tokens], acc[:])
 
         h0 = sbuf("h0", 2 * wide, BF16)
         h1 = sbuf("h1", 2 * wide, BF16, "h_late")
@@ -243,9 +238,7 @@ def tile_picked_route2_glusilu_p_kernel(
         nc.vector.tensor_tensor(gated0[:, :GROUP], y0[:, 0, :], gate_first[:], MULT)
         activate(6, 4)
         copy_linear(6, 0)
-        y10 = psum.tile([P, GROUP], F32, name="y10", tag="bank7")
-        rows10 = turned_product(y10, 1, 0, hw1, hs1)
-        turn_back(rows10, gated0[:, GROUP:], 3)
+        turned_unit(gated0[:, GROUP:], 0, hw1, hs1, (7, 2, 3, 6))
         for name, func, tile, bank in (("w1", SILU, silu[3], 5), ("w3", COPY, linear[3], 1)):
             product = first_product(name, 7, bank)
             for tokens in (slice(0, CHUNK // 2), slice(CHUNK // 2, CHUNK)):

@@ -1,7 +1,6 @@
 from contextlib import ExitStack
 
 import concourse.mybir as mybir
-from concourse.masks import make_identity
 
 K, T, S, H, N, U = 512, 2048, 1024, 512, 256, 2048
 FLOPS = 2 * S * (2 * K * H + H * N)
@@ -45,43 +44,35 @@ def tile_picked_route2_glusilu_p_kernel(
 
         offs_sb = keep.tile([P, S // PER_COL], U16, name="offs_sb")
         dst_sb = keep.tile([P, S // PER_COL], U16, name="dst_sb")
-        xs_table = keep.tile([P, T], U8, name="xs_table", align_bytes=64)
-        xw_table = keep.tile([P, T], U32, name="xw_table", align_bytes=64)
-        windows = [keep.tile([P, U], F32, name=f"window{m}", align_bytes=64) for m in range(N // P)]
+        xs_table = sbuf("xs_table", T, U8)
+        xw_table = sbuf("xw_table", T, U32)
+        windows = [sbuf(f"window{m}", U, F32) for m in range(N // P)]
 
         raw = {}
 
-        def load_weight_half(name, w, c):
+        def load_weight_piece(name, w, c):
             cols = PIECES[name][c]
             raw[name, c] = keep.tile(
                 [P, PACK, cols.stop - cols.start], F32, name=f"raw_{name}_{c}", tag=f"raw_{name}_{c}", align_bytes=64
             )
             nc.sync.dma_start(out=raw[name, c][:], in_=w.rearrange("(p j) c -> p j c", j=PACK)[:, :, cols])
 
-        gate_first = sbuf("gate_first", GROUP, F32)
-        gate_rest = sbuf("gate_rest", S - GROUP, F32)
-        gate_col = sbuf("gate_col", GROUP // CHUNK, F32)
-        identity = sbuf("identity", P, F32)
+        gate_sb = sbuf("gate_sb", S, F32)
         w2w = sbuf("w2w", N, U32)
         w2s = sbuf("w2s", N, U8)
         nc.vector.memset(xs_table[:].bitcast(I32), 0)
         nc.vector.memset(w2s[:].bitcast(I32), 0)
-        load_weight_half("w1", w1, 0)
+        load_weight_piece("w1", w1, 0)
         nc.sync.dma_start(offs_sb[:], offs)
         load_scale_rows((nc.sync, nc.scalar), xs_table, x_scales[0])
-        load_weight_half("w1", w1, 1)
+        load_weight_piece("w1", w1, 1)
         nc.sync.dma_start(out=xw_table[:].bitcast(I32), in_=x_words[0].rearrange("p c r -> p (c r)").bitcast(I32))
         for c in range(2):
-            load_weight_half("w3", w3, c)
+            load_weight_piece("w3", w3, c)
         load_scale_rows((nc.sync,), w2s, w2_scales[0])
         nc.sync.dma_start(out=w2w[:].bitcast(I32), in_=w2_words[0].rearrange("p c r -> p (c r)").bitcast(I32))
-        nc.sync.dma_start(out=gate_first[:], in_=gate[:, :GROUP])
         nc.sync.dma_start(dst_sb[:], dst)
-        with nc.allow_non_contiguous_dma(reason="one gate value a partition"):
-            nc.sync.dma_start(out=gate_col[:], in_=gate[0, GROUP : 2 * GROUP].rearrange("(c p) -> p c", p=P))
-        nc.sync.dma_start(out=gate_rest[:], in_=gate[:, GROUP:])
-        nc.vector.memset(identity[:], 0.0)
-        make_identity(nc, identity[:], nomemset=True)
+        nc.sync.dma_start(out=gate_sb[:], in_=gate)
 
         halves = (slice(0, U // 2), slice(U // 2, U))
         for half in halves:
@@ -102,9 +93,9 @@ def tile_picked_route2_glusilu_p_kernel(
 
         codes, scales, grouped = {}, {}, {}
         for name in ("w1", "w3"):
-            grouped[name] = keep.tile([P, H * PACK], BF16, name=f"grouped_{name}", tag=f"grouped_{name}", align_bytes=64)
-            codes[name] = keep.tile([P, H], U32, name=f"codes_{name}", align_bytes=64)
-            scales[name] = keep.tile([P, H], U8, name=f"scales_{name}", align_bytes=64)
+            grouped[name] = sbuf(f"grouped_{name}", H * PACK, BF16)
+            codes[name] = sbuf(f"codes_{name}", H, U32)
+            scales[name] = sbuf(f"scales_{name}", H, U8)
 
         def deal(copy, name, c, tiles):
             dealt = grouped[name][:].rearrange("p (t m j) -> p m j t", t=PACK, j=PACK)
@@ -132,8 +123,8 @@ def tile_picked_route2_glusilu_p_kernel(
             quantise("w1", tiles)
         gather(xw, xw_table, U32, 0, LATE, "xw0")
         gather(xw, xw_table, U32, LATE, S - 2 * LATE, "xw1")
-        deal(nc.scalar.copy, "w3", 0, tile_pairs[0])
-        deal(gpsimd_cast, "w3", 0, tile_pairs[1])
+        for tiles in tile_pairs:
+            deal(gpsimd_cast, "w3", 0, tiles)
         for tiles in tile_pairs:
             deal(nc.vector.tensor_copy, "w3", 1, tiles)
         for tiles in tile_pairs:
@@ -156,114 +147,80 @@ def tile_picked_route2_glusilu_p_kernel(
             return acc[:].rearrange("p t n -> p n t")
 
         wide = CHUNK * PACK
-        silu_early = sbuf("silu_early", 4 * wide, F32, "raw_w3_0")
-        silu = [silu_early[:, : 2 * wide], silu_early[:, 2 * wide :]]
-        silu += [sbuf(f"silu{g}", 2 * wide, F32)[:] for g in (2, 3)]
-        linear = {g: sbuf(f"linear{g}", 2 * wide, F32) for g in (2, 3)}
+        groups = S // GROUP
+        silu = [sbuf(f"silu{c}", wide, F32) for c in range(S // CHUNK)]
+        hidden = [sbuf(f"hidden{g}", 2 * wide, BF16) for g in range(groups)]
+        gated = [sbuf(f"gated{m}", S, F32) for m in range(N // P)]
+        y = {}
 
-        def part(tile, i):
-            return tile[:, i * wide : (i + 1) * wide].rearrange("p (n t) -> p n t", t=PACK)
+        def by_token(ap):
+            return ap.rearrange("p (n t) -> p n t", t=PACK)
 
-        def activate(c, bank):
-            nc.scalar.activation(part(silu[c // 2], c % 2), first_product("w1", c, bank), SILU)
+        def activate(c):
+            nc.scalar.activation(by_token(silu[c][:]), first_product("w1", c, c % 3), SILU)
 
-        def multiply(h, c, bank):
-            nc.vector.tensor_tensor(part(h, c % 2), first_product("w3", c, bank), part(silu[c // 2], c % 2), MULT)
+        def multiply(c):
+            target = hidden[c // 2][:, (c % 2) * wide : (c % 2 + 1) * wide]
+            nc.vector.tensor_tensor(by_token(target), first_product("w3", c, 3 + c % 3), by_token(silu[c][:]), MULT)
 
-        def copy_linear(c, bank):
-            nc.scalar.copy(part(linear[c // 2], c % 2), first_product("w3", c, bank))
+        def second_product(g):
+            hw = sbuf(f"hw{g}", GROUP, U32)
+            hs = sbuf(f"hs{g}", GROUP, U8)
+            nc.vector.quantize_mx(out=hw[:].bitcast(FP8X4), scales=hs[:], in_=hidden[g][:])
+            acc = psum.tile([P, N // P, GROUP], F32, name=f"y{g}", tag=f"bank{(6, 7, 0, 1)[g]}")
+            for m in range(N // P):
+                cols = slice(m * P, (m + 1) * P)
+                nc.tensor.matmul_mx(
+                    out=acc[:, m, :],
+                    lhsT=w2w[:, cols].bitcast(FP8X4),
+                    lhsT_scale=w2s[:, cols],
+                    rhs=hw[:].bitcast(FP8X4),
+                    rhs_scale=hs[:],
+                    start=True,
+                    stop=True,
+                )
+            y[g] = acc
 
-        def quantise_h(name, h, tokens):
-            hw = sbuf(f"hw{name}", tokens, U32)
-            hs = sbuf(f"hs{name}", tokens, U8)
-            nc.vector.quantize_mx(out=hw[:].bitcast(FP8X4), scales=hs[:], in_=h[:])
-            return hw[:], hs[:]
-
-        def second_product(acc, m, hw, hs):
-            cols = slice(m * P, (m + 1) * P)
-            nc.tensor.matmul_mx(
-                out=acc,
-                lhsT=w2w[:, cols].bitcast(FP8X4),
-                lhsT_scale=w2s[:, cols],
-                rhs=hw.bitcast(FP8X4),
-                rhs_scale=hs,
-                start=True,
-                stop=True,
-            )
+        def apply_gate(m, g):
+            tokens = slice(g * GROUP, (g + 1) * GROUP)
+            nc.vector.tensor_tensor(gated[m][:, tokens], y[g][:, m, :], gate_sb[:, tokens], MULT)
 
         def places(m, first, count):
             return windows[m][:].indirect(dst_sb[:, first // PER_COL : (first + count) // PER_COL])
 
-        def turned_unit(y, m, hw, hs, banks):
-            cols = slice(m * P, (m + 1) * P)
-            rows = sbuf("rows", GROUP, F32)
-            chunks = [slice(i * CHUNK, (i + 1) * CHUNK) for i in range(GROUP // CHUNK)]
-            for i, tokens in enumerate(chunks):
-                acc = psum.tile([P, CHUNK], F32, name=f"turned{i}", tag=f"bank{banks[i]}")
-                nc.tensor.matmul_mx(
-                    out=acc[:],
-                    lhsT=hw[:, tokens].bitcast(FP8X4),
-                    lhsT_scale=hs[:, tokens],
-                    rhs=w2w[:, cols].bitcast(FP8X4),
-                    rhs_scale=w2s[:, cols],
-                    start=True,
-                    stop=True,
-                )
-                nc.scalar.activation(rows[:, tokens], acc[:], COPY, scale=gate_col[:, i : i + 1])
-            for i, tokens in enumerate(chunks):
-                acc = psum.tile([P, CHUNK], F32, name=f"back{i}", tag=f"bank{banks[2 + i]}")
-                nc.tensor.transpose(acc[:], rows[:, tokens], identity[:])
-                nc.scalar.copy(y[:, tokens], acc[:])
+        def scalar_scatter(m, first, count):
+            nc.scalar.activation(places(m, first, count), gated[m][:, first : first + count], COPY)
 
-        h0 = sbuf("h0", 2 * wide, BF16)
-        h1 = sbuf("h1", 2 * wide, BF16, "h_late")
-        for c in range(4):
-            activate(c, c)
-        multiply(h0, 0, 4)
-        multiply(h0, 1, 5)
-        multiply(h1, 2, 6)
-        activate(4, 0)
-        copy_linear(4, 1)
-        activate(5, 3)
-        copy_linear(5, 2)
-        hw0, hs0 = quantise_h("0", h0, GROUP)
-        multiply(h1, 3, 7)
-        y0 = psum.tile([P, 2, GROUP], F32, name="y0", tag="bank6")
-        for m in (1, 0):
-            second_product(y0[:, m, :], m, hw0, hs0)
-        gated0 = sbuf("gated0", 2 * GROUP, F32)
-        gated1 = sbuf("gated1", GROUP, F32)
-        nc.vector.tensor_tensor(gated1[:], y0[:, 1, :], gate_first[:], MULT)
-        hw1, hs1 = quantise_h("1", h1, GROUP)
-        nc.vector.tensor_tensor(gated0[:, :GROUP], y0[:, 0, :], gate_first[:], MULT)
-        activate(6, 4)
-        copy_linear(6, 0)
-        turned_unit(gated0[:, GROUP:], 0, hw1, hs1, (7, 2, 3, 6))
-        for name, func, tile, bank in (("w1", SILU, silu[3], 5), ("w3", COPY, linear[3], 1)):
-            product = first_product(name, 7, bank)
-            for tokens in (slice(0, CHUNK // 2), slice(CHUNK // 2, CHUNK)):
-                nc.scalar.activation(part(tile, 1)[:, tokens], product[:, tokens], func)
-
-        h23 = sbuf("h23", 4 * wide, BF16, "h_late")
-        for g in (2, 3):
-            nc.gpsimd.tensor_tensor(h23[:, (g - 2) * 2 * wide : (g - 1) * 2 * wide], linear[g][:], silu[g], MULT)
-
-        nc.vector.tensor_copy(places(1, 0, GROUP), gated1[:])
-        nc.vector.tensor_copy(places(0, 0, 2 * GROUP), gated0[:])
-
-        hw23, hs23 = quantise_h("23", h23, 2 * GROUP)
-        acc11 = psum.tile([P, GROUP], F32, name="acc11", tag="bank3")
-        second_product(acc11[:], 1, hw1, hs1)
-        y11 = sbuf("y11", GROUP, F32, "linear3")
-        nc.scalar.copy(y11[:], acc11[:])
-        nc.vector.tensor_tensor(places(1, GROUP, GROUP), y11[:], gate_rest[:, :GROUP], MULT)
-        for m in range(2):
-            y = sbuf(f"y23_{m}", 2 * GROUP, F32)
-            for i in range(2):
-                tokens = slice(i * GROUP, (i + 1) * GROUP)
-                acc = psum.tile([P, GROUP], F32, name=f"acc23_{m}_{i}", tag=f"bank{2 * m + i}")
-                second_product(acc[:], m, hw23[:, tokens], hs23[:, tokens])
-                nc.scalar.copy(y[:, tokens], acc[:])
-            nc.vector.tensor_tensor(places(m, 2 * GROUP, 2 * GROUP), y[:], gate_rest[:, GROUP:], MULT)
+        def store(m):
             for queue, half in zip((nc.sync, nc.scalar), halves):
                 queue.dma_start(out=out[m * P : (m + 1) * P, half], in_=windows[m][:, half])
+
+        for c in range(S // CHUNK):
+            activate(c)
+        for c in range(3):
+            multiply(c)
+        second_product(0)
+        multiply(3)
+        apply_gate(0, 0)
+        scalar_scatter(0, 0, GROUP)
+        second_product(1)
+        apply_gate(1, 0)
+        scalar_scatter(1, 0, GROUP)
+        multiply(4)
+        multiply(5)
+        apply_gate(0, 1)
+        scalar_scatter(0, GROUP, GROUP)
+        multiply(6)
+        second_product(2)
+        multiply(7)
+        apply_gate(0, 2)
+        scalar_scatter(0, 2 * GROUP, GROUP)
+        second_product(3)
+        apply_gate(1, 1)
+        apply_gate(1, 2)
+        apply_gate(0, 3)
+        scalar_scatter(0, 3 * GROUP, GROUP)
+        apply_gate(1, 3)
+        store(0)
+        nc.vector.tensor_copy(places(1, GROUP, S - GROUP), gated[1][:, GROUP:])
+        store(1)

@@ -21,9 +21,13 @@ P = 128
 PACK = 4
 CHUNK = 128
 GROUP = 256
-PIECES = {"w1": (slice(0, H // 4), slice(H // 4, H)), "w3": (slice(0, H // 2), slice(H // 2, H))}
+PIECES = {"w1": (slice(0, H // 2), slice(H // 2, H)), "w3": (slice(0, H // 2), slice(H // 2, H))}
 PER_COL = 16
 LATE = 256
+GROUPS = (slice(0, 256), slice(256, 640), slice(640, S))
+SILU_BANKS = (0, 1, 2, 3, 4, 3, 4, 5)
+LINEAR_BANKS = (5, 6, 7, 0, 1, 2, 1, 6)
+OUT_BANKS = ((1, 2), (6, 7), (0, 3))
 
 
 def load_scale_rows(queues, plane, rows):
@@ -57,7 +61,8 @@ def tile_picked_route2_glusilu_p_kernel(
             )
             nc.sync.dma_start(out=raw[name, c][:], in_=w.rearrange("(p j) c -> p j c", j=PACK)[:, :, cols])
 
-        gate_sb = sbuf("gate_sb", S, F32)
+        gate_first = sbuf("gate_first", GROUP, F32)
+        gate_rest = sbuf("gate_rest", S - GROUP, F32)
         w2w = sbuf("w2w", N, U32)
         w2s = sbuf("w2s", N, U8)
         nc.vector.memset(xs_table[:].bitcast(I32), 0)
@@ -71,8 +76,9 @@ def tile_picked_route2_glusilu_p_kernel(
             load_weight_piece("w3", w3, c)
         load_scale_rows((nc.sync,), w2s, w2_scales[0])
         nc.sync.dma_start(out=w2w[:].bitcast(I32), in_=w2_words[0].rearrange("p c r -> p (c r)").bitcast(I32))
+        nc.sync.dma_start(out=gate_first[:], in_=gate[:, :GROUP])
         nc.sync.dma_start(dst_sb[:], dst)
-        nc.sync.dma_start(out=gate_sb[:], in_=gate)
+        nc.sync.dma_start(out=gate_rest[:], in_=gate[:, GROUP:])
 
         halves = (slice(0, U // 2), slice(U // 2, U))
         for half in halves:
@@ -122,14 +128,12 @@ def tile_picked_route2_glusilu_p_kernel(
             deal(nc.scalar.copy, "w1", 1, tiles)
             quantise("w1", tiles)
         gather(xw, xw_table, U32, 0, LATE, "xw0")
-        gather(xw, xw_table, U32, LATE, S - 2 * LATE, "xw1")
-        for tiles in tile_pairs:
-            deal(gpsimd_cast, "w3", 0, tiles)
-        for tiles in tile_pairs:
-            deal(nc.vector.tensor_copy, "w3", 1, tiles)
+        gather(xw, xw_table, U32, LATE, S - LATE, "xw1")
+        for c in range(2):
+            deal(nc.scalar.copy, "w3", c, tile_pairs[0])
+            deal(gpsimd_cast, "w3", c, tile_pairs[1])
         for tiles in tile_pairs:
             quantise("w3", tiles)
-        gather(xw, xw_table, U32, S - LATE, LATE, "raw_w3_1")
 
         def first_product(name, c, bank):
             acc = psum.tile([P, PACK, CHUNK], F32, name=f"acc_{name}_{c}", tag=f"bank{bank}")
@@ -147,80 +151,85 @@ def tile_picked_route2_glusilu_p_kernel(
             return acc[:].rearrange("p t n -> p n t")
 
         wide = CHUNK * PACK
-        groups = S // GROUP
-        silu = [sbuf(f"silu{c}", wide, F32) for c in range(S // CHUNK)]
-        hidden = [sbuf(f"hidden{g}", 2 * wide, BF16) for g in range(groups)]
+        silu = []
+        for name, tag, count in (("silu_first", "raw_w3_0", 2), ("silu_next", "raw_w3_1", 2), ("silu_rest", None, 4)):
+            tile = sbuf(name, count * wide, F32, tag)
+            silu += [tile[:, i * wide : (i + 1) * wide] for i in range(count)]
+        hidden = sbuf("hidden", S * PACK, BF16)
+        hw = sbuf("hw", S, U32)
+        hs = sbuf("hs", S, U8)
         gated = [sbuf(f"gated{m}", S, F32) for m in range(N // P)]
-        y = {}
 
         def by_token(ap):
             return ap.rearrange("p (n t) -> p n t", t=PACK)
 
         def activate(c):
-            nc.scalar.activation(by_token(silu[c][:]), first_product("w1", c, c % 3), SILU)
+            nc.scalar.activation(by_token(silu[c]), first_product("w1", c, SILU_BANKS[c]), SILU)
 
         def multiply(c):
-            target = hidden[c // 2][:, (c % 2) * wide : (c % 2 + 1) * wide]
-            nc.vector.tensor_tensor(by_token(target), first_product("w3", c, 3 + c % 3), by_token(silu[c][:]), MULT)
+            target = hidden[:, c * wide : (c + 1) * wide]
+            nc.vector.tensor_tensor(by_token(target), first_product("w3", c, LINEAR_BANKS[c]), by_token(silu[c]), MULT)
 
-        def second_product(g):
-            hw = sbuf(f"hw{g}", GROUP, U32)
-            hs = sbuf(f"hs{g}", GROUP, U8)
-            nc.vector.quantize_mx(out=hw[:].bitcast(FP8X4), scales=hs[:], in_=hidden[g][:])
-            acc = psum.tile([P, N // P, GROUP], F32, name=f"y{g}", tag=f"bank{(6, 7, 0, 1)[g]}")
-            for m in range(N // P):
-                cols = slice(m * P, (m + 1) * P)
+        def quantise_hidden(first, last):
+            tokens = slice(first * CHUNK, last * CHUNK)
+            nc.vector.quantize_mx(out=hw[:, tokens].bitcast(FP8X4), scales=hs[:, tokens], in_=hidden[:, first * wide : last * wide])
+
+        def gated_product(m, g):
+            group = GROUPS[g]
+            cols = slice(m * P, (m + 1) * P)
+            y = psum.tile([P, group.stop - group.start], F32, name=f"y{m}{g}", tag=f"bank{OUT_BANKS[g][m]}")
+            for first in range(group.start, group.stop, GROUP):
+                tokens = slice(first, min(first + GROUP, group.stop))
                 nc.tensor.matmul_mx(
-                    out=acc[:, m, :],
+                    out=y[:, tokens.start - group.start : tokens.stop - group.start],
                     lhsT=w2w[:, cols].bitcast(FP8X4),
                     lhsT_scale=w2s[:, cols],
-                    rhs=hw[:].bitcast(FP8X4),
-                    rhs_scale=hs[:],
+                    rhs=hw[:, tokens].bitcast(FP8X4),
+                    rhs_scale=hs[:, tokens],
                     start=True,
                     stop=True,
                 )
-            y[g] = acc
+            weights = gate_rest[:, group.start - GROUP : group.stop - GROUP] if g else gate_first[:]
+            nc.vector.tensor_tensor(gated[m][:, group], y[:], weights, MULT)
 
-        def apply_gate(m, g):
-            tokens = slice(g * GROUP, (g + 1) * GROUP)
-            nc.vector.tensor_tensor(gated[m][:, tokens], y[g][:, m, :], gate_sb[:, tokens], MULT)
+        def places(m, tokens):
+            return windows[m][:].indirect(dst_sb[:, tokens.start // PER_COL : tokens.stop // PER_COL])
 
-        def places(m, first, count):
-            return windows[m][:].indirect(dst_sb[:, first // PER_COL : (first + count) // PER_COL])
+        def scalar_scatter(m, g):
+            nc.scalar.activation(places(m, GROUPS[g]), gated[m][:, GROUPS[g]], COPY)
 
-        def scalar_scatter(m, first, count):
-            nc.scalar.activation(places(m, first, count), gated[m][:, first : first + count], COPY)
+        def store(queue, m):
+            queue.dma_start(out=out[m * P : (m + 1) * P, :], in_=windows[m][:])
 
-        def store(m):
-            for queue, half in zip((nc.sync, nc.scalar), halves):
-                queue.dma_start(out=out[m * P : (m + 1) * P, half], in_=windows[m][:, half])
-
-        for c in range(S // CHUNK):
+        for c in range(5):
             activate(c)
-        for c in range(3):
-            multiply(c)
-        second_product(0)
+        multiply(0)
+        multiply(1)
+        activate(5)
+        quantise_hidden(0, 1)
+        quantise_hidden(1, 2)
+        multiply(2)
+        activate(6)
+        activate(7)
+        gated_product(0, 0)
+        scalar_scatter(0, 0)
         multiply(3)
-        apply_gate(0, 0)
-        scalar_scatter(0, 0, GROUP)
-        second_product(1)
-        apply_gate(1, 0)
-        scalar_scatter(1, 0, GROUP)
         multiply(4)
+        gated_product(1, 0)
+        scalar_scatter(1, 0)
+        quantise_hidden(2, 5)
         multiply(5)
-        apply_gate(0, 1)
-        scalar_scatter(0, GROUP, GROUP)
+        gated_product(0, 1)
+        scalar_scatter(0, 1)
         multiply(6)
-        second_product(2)
         multiply(7)
-        apply_gate(0, 2)
-        scalar_scatter(0, 2 * GROUP, GROUP)
-        second_product(3)
-        apply_gate(1, 1)
-        apply_gate(1, 2)
-        apply_gate(0, 3)
-        scalar_scatter(0, 3 * GROUP, GROUP)
-        apply_gate(1, 3)
-        store(0)
-        nc.vector.tensor_copy(places(1, GROUP, S - GROUP), gated[1][:, GROUP:])
-        store(1)
+        quantise_hidden(5, 7)
+        quantise_hidden(7, 8)
+        gated_product(1, 1)
+        gated_product(1, 2)
+        gated_product(0, 2)
+        scalar_scatter(0, 2)
+        store(nc.sync, 0)
+        rest = slice(GROUP, S)
+        nc.vector.tensor_copy(places(1, rest), gated[1][:, rest])
+        store(nc.scalar, 1)

@@ -21,13 +21,13 @@ P = 128
 PACK = 4
 CHUNK = 128
 GROUP = 256
-PIECES = {"w1": (slice(0, H // 2), slice(H // 2, H)), "w3": (slice(0, H // 2), slice(H // 2, H))}
+PIECES = {"w1": (slice(0, H // 4), slice(H // 4, H)), "w3": (slice(0, H // 2), slice(H // 2, H))}
 PER_COL = 16
 LATE = 256
-GROUPS = (slice(0, 256), slice(256, 640), slice(640, S))
-SILU_BANKS = (0, 1, 2, 3, 4, 3, 4, 5)
-LINEAR_BANKS = (5, 6, 7, 0, 1, 2, 1, 6)
-OUT_BANKS = ((1, 2), (6, 7), (0, 3))
+GROUPS = (slice(0, 256), slice(256, 640), slice(640, 896), slice(896, S))
+SILU_BANKS = (0, 1, 2, 3, 4, 5, 7, 0)
+LINEAR_BANKS = (5, 6, 1, 2, 3, 4, 6, 1)
+OUT_BANKS = ((7, 0), (5, 2), (3, 7), (0, 4))
 
 
 def load_scale_rows(queues, plane, rows):
@@ -56,9 +56,8 @@ def tile_picked_route2_glusilu_p_kernel(
 
         def load_weight_piece(name, w, c):
             cols = PIECES[name][c]
-            raw[name, c] = keep.tile(
-                [P, PACK, cols.stop - cols.start], F32, name=f"raw_{name}_{c}", tag=f"raw_{name}_{c}", align_bytes=64
-            )
+            shape = [P, PACK, cols.stop - cols.start]
+            raw[name, c] = keep.tile(shape, F32, name=f"raw_{name}_{c}", tag=f"raw_{name}_{c}", align_bytes=64)
             nc.sync.dma_start(out=raw[name, c][:], in_=w.rearrange("(p j) c -> p j c", j=PACK)[:, :, cols])
 
         gate_first = sbuf("gate_first", GROUP, F32)
@@ -88,14 +87,13 @@ def tile_picked_route2_glusilu_p_kernel(
 
         xw, xs = {}, {}
 
-        def gather(into, table, dtype, first, count, tag):
-            picked = keep.tile([P, count], dtype, name=tag + "_picked", tag=tag, align_bytes=64)
+        def gather(into, table, first, count, picked):
             cols = slice(first // PER_COL, (first + count) // PER_COL)
             nc.vector.tensor_copy(picked[:], table[:].indirect(offs_sb[:, cols]))
             for c in range(count // CHUNK):
                 into[first // CHUNK + c] = picked[:, c * CHUNK : (c + 1) * CHUNK]
 
-        gather(xs, xs_table, U8, 0, S, "xs")
+        gather(xs, xs_table, 0, S, sbuf("xs", S, U8))
 
         codes, scales, grouped = {}, {}, {}
         for name in ("w1", "w3"):
@@ -127,13 +125,15 @@ def tile_picked_route2_glusilu_p_kernel(
         for tiles in tile_pairs:
             deal(nc.scalar.copy, "w1", 1, tiles)
             quantise("w1", tiles)
-        gather(xw, xw_table, U32, 0, LATE, "xw0")
-        gather(xw, xw_table, U32, LATE, S - LATE, "xw1")
-        for c in range(2):
-            deal(nc.scalar.copy, "w3", c, tile_pairs[0])
-            deal(gpsimd_cast, "w3", c, tile_pairs[1])
+        gather(xw, xw_table, 0, LATE, sbuf("xw0", LATE, U32))
+        gather(xw, xw_table, LATE, S - 2 * LATE, sbuf("xw1", S - 2 * LATE, U32))
+        deal(nc.scalar.copy, "w3", 0, tile_pairs[0])
+        deal(gpsimd_cast, "w3", 0, tile_pairs[1])
+        for tiles in tile_pairs:
+            deal(nc.vector.tensor_copy, "w3", 1, tiles)
         for tiles in tile_pairs:
             quantise("w3", tiles)
+        gather(xw, xw_table, S - LATE, LATE, sbuf("xw2", LATE, U32, "raw_w3_1"))
 
         def first_product(name, c, bank):
             acc = psum.tile([P, PACK, CHUNK], F32, name=f"acc_{name}_{c}", tag=f"bank{bank}")
@@ -151,14 +151,18 @@ def tile_picked_route2_glusilu_p_kernel(
             return acc[:].rearrange("p t n -> p n t")
 
         wide = CHUNK * PACK
-        silu = []
-        for name, tag, count in (("silu_first", "raw_w3_0", 2), ("silu_next", "raw_w3_1", 2), ("silu_rest", None, 4)):
-            tile = sbuf(name, count * wide, F32, tag)
-            silu += [tile[:, i * wide : (i + 1) * wide] for i in range(count)]
-        hidden = sbuf("hidden", S * PACK, BF16)
+        silu_all = sbuf("silu_all", S * PACK, F32, "raw_w3_0")
+        silu = [silu_all[:, c * wide : (c + 1) * wide] for c in range(S // CHUNK)]
+        hidden = {0: sbuf("hidden_early", 5 * wide, BF16)}
         hw = sbuf("hw", S, U32)
         hs = sbuf("hs", S, U8)
         gated = [sbuf(f"gated{m}", S, F32) for m in range(N // P)]
+
+        y = {}
+
+        def hidden_part(first, last):
+            base = max(b for b in hidden if b <= first)
+            return hidden[base][:, (first - base) * wide : (last - base) * wide]
 
         def by_token(ap):
             return ap.rearrange("p (n t) -> p n t", t=PACK)
@@ -167,21 +171,21 @@ def tile_picked_route2_glusilu_p_kernel(
             nc.scalar.activation(by_token(silu[c]), first_product("w1", c, SILU_BANKS[c]), SILU)
 
         def multiply(c):
-            target = hidden[:, c * wide : (c + 1) * wide]
+            target = hidden_part(c, c + 1)
             nc.vector.tensor_tensor(by_token(target), first_product("w3", c, LINEAR_BANKS[c]), by_token(silu[c]), MULT)
 
         def quantise_hidden(first, last):
             tokens = slice(first * CHUNK, last * CHUNK)
-            nc.vector.quantize_mx(out=hw[:, tokens].bitcast(FP8X4), scales=hs[:, tokens], in_=hidden[:, first * wide : last * wide])
+            nc.vector.quantize_mx(out=hw[:, tokens].bitcast(FP8X4), scales=hs[:, tokens], in_=hidden_part(first, last))
 
-        def gated_product(m, g):
+        def second_product(m, g):
             group = GROUPS[g]
             cols = slice(m * P, (m + 1) * P)
-            y = psum.tile([P, group.stop - group.start], F32, name=f"y{m}{g}", tag=f"bank{OUT_BANKS[g][m]}")
+            y[m, g] = psum.tile([P, group.stop - group.start], F32, name=f"y{m}{g}", tag=f"bank{OUT_BANKS[g][m]}")
             for first in range(group.start, group.stop, GROUP):
                 tokens = slice(first, min(first + GROUP, group.stop))
                 nc.tensor.matmul_mx(
-                    out=y[:, tokens.start - group.start : tokens.stop - group.start],
+                    out=y[m, g][:, tokens.start - group.start : tokens.stop - group.start],
                     lhsT=w2w[:, cols].bitcast(FP8X4),
                     lhsT_scale=w2s[:, cols],
                     rhs=hw[:, tokens].bitcast(FP8X4),
@@ -189,14 +193,19 @@ def tile_picked_route2_glusilu_p_kernel(
                     start=True,
                     stop=True,
                 )
+
+        def gated_product(m, g):
+            group = GROUPS[g]
+            if (m, g) not in y:
+                second_product(m, g)
             weights = gate_rest[:, group.start - GROUP : group.stop - GROUP] if g else gate_first[:]
-            nc.vector.tensor_tensor(gated[m][:, group], y[:], weights, MULT)
+            nc.vector.tensor_tensor(gated[m][:, group], y[m, g][:], weights, MULT)
 
         def places(m, tokens):
             return windows[m][:].indirect(dst_sb[:, tokens.start // PER_COL : tokens.stop // PER_COL])
 
-        def scalar_scatter(m, g):
-            nc.scalar.activation(places(m, GROUPS[g]), gated[m][:, GROUPS[g]], COPY)
+        def scalar_scatter(m, tokens):
+            nc.scalar.activation(places(m, tokens), gated[m][:, tokens], COPY)
 
         def store(queue, m):
             queue.dma_start(out=out[m * P : (m + 1) * P, :], in_=windows[m][:])
@@ -205,30 +214,33 @@ def tile_picked_route2_glusilu_p_kernel(
             activate(c)
         multiply(0)
         multiply(1)
-        activate(5)
-        quantise_hidden(0, 1)
-        quantise_hidden(1, 2)
-        multiply(2)
         activate(6)
         activate(7)
-        gated_product(0, 0)
-        scalar_scatter(0, 0)
+        quantise_hidden(0, 1)
+        quantise_hidden(1, 2)
+        second_product(0, 0)
+        multiply(2)
+        activate(5)
         multiply(3)
+        gated_product(0, 0)
+        scalar_scatter(0, GROUPS[0])
         multiply(4)
         gated_product(1, 0)
-        scalar_scatter(1, 0)
+        scalar_scatter(1, GROUPS[0])
         quantise_hidden(2, 5)
+        hidden[5] = sbuf("hidden_late", 3 * wide, BF16, "gate_first")
         multiply(5)
-        gated_product(0, 1)
-        scalar_scatter(0, 1)
         multiply(6)
-        multiply(7)
+        gated_product(0, 1)
+        scalar_scatter(0, GROUPS[1])
         quantise_hidden(5, 7)
-        quantise_hidden(7, 8)
+        multiply(7)
         gated_product(1, 1)
-        gated_product(1, 2)
-        gated_product(0, 2)
-        scalar_scatter(0, 2)
+        quantise_hidden(7, 8)
+        for g in (2, 3):
+            for m in range(N // P):
+                gated_product(m, g)
+        scalar_scatter(0, slice(GROUPS[2].start, S))
         store(nc.sync, 0)
         rest = slice(GROUP, S)
         nc.vector.tensor_copy(places(1, rest), gated[1][:, rest])

@@ -23,9 +23,11 @@ CHUNK = 128
 GROUP = 256
 PIECES = {"w1": (slice(0, H // 4), slice(H // 4, H)), "w3": (slice(0, H // 2), slice(H // 2, H))}
 PER_COL = 16
-LATE = 256
+EARLY = 256
+LATE = 128
+SILU_BYTES = CHUNK * PACK * 4
 GROUPS = (slice(0, 256), slice(256, 640), slice(640, 896), slice(896, S))
-SILU_BANKS = (0, 1, 2, 3, 4, 5, 7, 0)
+SILU_BANKS = (0, 1, 2, 3, 4, 5, 6, 0)
 LINEAR_BANKS = (5, 6, 1, 2, 3, 4, 6, 1)
 OUT_BANKS = ((7, 0), (5, 2), (3, 7), (0, 4))
 
@@ -42,6 +44,7 @@ def tile_picked_route2_glusilu_p_kernel(
     with ExitStack() as ctx:
         keep = ctx.enter_context(tc.tile_pool(name="keep", bufs=1))
         psum = ctx.enter_context(tc.psum_pool(name="psum", bufs=1))
+        shared = ctx.enter_context(tc.tile_pool(name="shared", bufs=1))
 
         def sbuf(name, columns, dtype, tag=None):
             return keep.tile([P, columns], dtype, name=name, tag=tag or name, align_bytes=64)
@@ -57,7 +60,10 @@ def tile_picked_route2_glusilu_p_kernel(
         def load_weight_piece(name, w, c):
             cols = PIECES[name][c]
             shape = [P, PACK, cols.stop - cols.start]
-            raw[name, c] = keep.tile(shape, F32, name=f"raw_{name}_{c}", tag=f"raw_{name}_{c}", align_bytes=64)
+            if (name, c) == ("w3", 0):
+                raw[name, c] = shared.tile(shape, F32, name="raw_w3_0", align_bytes=64, offset=SILU_BYTES - 64)
+            else:
+                raw[name, c] = keep.tile(shape, F32, name=f"raw_{name}_{c}", tag=f"raw_{name}_{c}", align_bytes=64)
             nc.sync.dma_start(out=raw[name, c][:], in_=w.rearrange("(p j) c -> p j c", j=PACK)[:, :, cols])
 
         gate_first = sbuf("gate_first", GROUP, F32)
@@ -125,8 +131,8 @@ def tile_picked_route2_glusilu_p_kernel(
         for tiles in tile_pairs:
             deal(nc.scalar.copy, "w1", 1, tiles)
             quantise("w1", tiles)
-        gather(xw, xw_table, 0, LATE, sbuf("xw0", LATE, U32))
-        gather(xw, xw_table, LATE, S - 2 * LATE, sbuf("xw1", S - 2 * LATE, U32))
+        gather(xw, xw_table, 0, EARLY, sbuf("xw0", EARLY, U32))
+        gather(xw, xw_table, EARLY, S - EARLY - LATE, sbuf("xw1", S - EARLY - LATE, U32))
         deal(nc.scalar.copy, "w3", 0, tile_pairs[0])
         deal(gpsimd_cast, "w3", 0, tile_pairs[1])
         for tiles in tile_pairs:
@@ -151,9 +157,10 @@ def tile_picked_route2_glusilu_p_kernel(
             return acc[:].rearrange("p t n -> p n t")
 
         wide = CHUNK * PACK
-        silu_all = sbuf("silu_all", S * PACK, F32, "raw_w3_0")
-        silu = [silu_all[:, c * wide : (c + 1) * wide] for c in range(S // CHUNK)]
-        hidden = {0: sbuf("hidden_early", 5 * wide, BF16)}
+        silu = [shared.tile([P, wide], F32, name=f"silu{c}", align_bytes=64, offset=c * SILU_BYTES)[:] for c in range(2)]
+        silu_rest = shared.tile([P, 6 * wide], F32, name="silu_rest", align_bytes=64, offset=2 * SILU_BYTES)
+        silu += [silu_rest[:, c * wide : (c + 1) * wide] for c in range(6)]
+        hidden = {0: sbuf("hidden_first", 2 * wide, BF16)}
         hw = sbuf("hw", S, U32)
         hs = sbuf("hs", S, U8)
         gated = [sbuf(f"gated{m}", S, F32) for m in range(N // P)]
@@ -170,9 +177,13 @@ def tile_picked_route2_glusilu_p_kernel(
         def activate(c):
             nc.scalar.activation(by_token(silu[c]), first_product("w1", c, SILU_BANKS[c]), SILU)
 
-        def multiply(c):
-            target = hidden_part(c, c + 1)
-            nc.vector.tensor_tensor(by_token(target), first_product("w3", c, LINEAR_BANKS[c]), by_token(silu[c]), MULT)
+        linear = {}
+
+        def multiply(c, tokens=slice(0, CHUNK)):
+            if c not in linear:
+                linear[c] = first_product("w3", c, LINEAR_BANKS[c])
+            target = by_token(hidden_part(c, c + 1))
+            nc.vector.tensor_tensor(target[:, tokens], linear[c][:, tokens], by_token(silu[c])[:, tokens], MULT)
 
         def quantise_hidden(first, last):
             tokens = slice(first * CHUNK, last * CHUNK)
@@ -201,6 +212,10 @@ def tile_picked_route2_glusilu_p_kernel(
             weights = gate_rest[:, group.start - GROUP : group.stop - GROUP] if g else gate_first[:]
             nc.vector.tensor_tensor(gated[m][:, group], y[m, g][:], weights, MULT)
 
+        def plain_product(g):
+            second_product(1, g)
+            nc.vector.tensor_copy(gated[1][:, GROUPS[g]], y[1, g][:])
+
         def places(m, tokens):
             return windows[m][:].indirect(dst_sb[:, tokens.start // PER_COL : tokens.stop // PER_COL])
 
@@ -214,16 +229,18 @@ def tile_picked_route2_glusilu_p_kernel(
             activate(c)
         multiply(0)
         multiply(1)
-        activate(6)
         activate(7)
         quantise_hidden(0, 1)
         quantise_hidden(1, 2)
         second_product(0, 0)
+        hidden[2] = shared.tile([P, 3 * wide], BF16, name="hidden_next", align_bytes=64, offset=SILU_BYTES // 2)
         multiply(2)
         activate(5)
-        multiply(3)
+        activate(6)
+        multiply(3, slice(0, CHUNK // 2))
         gated_product(0, 0)
         scalar_scatter(0, GROUPS[0])
+        multiply(3, slice(CHUNK // 2, CHUNK))
         multiply(4)
         gated_product(1, 0)
         scalar_scatter(1, GROUPS[0])
@@ -233,15 +250,16 @@ def tile_picked_route2_glusilu_p_kernel(
         multiply(6)
         gated_product(0, 1)
         scalar_scatter(0, GROUPS[1])
-        quantise_hidden(5, 7)
         multiply(7)
-        gated_product(1, 1)
+        quantise_hidden(5, 7)
         quantise_hidden(7, 8)
-        for g in (2, 3):
-            for m in range(N // P):
-                gated_product(m, g)
+        plain_product(1)
+        gated_product(0, 2)
+        plain_product(2)
+        plain_product(3)
+        gated_product(0, 3)
         scalar_scatter(0, slice(GROUPS[2].start, S))
         store(nc.sync, 0)
         rest = slice(GROUP, S)
-        nc.vector.tensor_copy(places(1, rest), gated[1][:, rest])
+        nc.vector.tensor_tensor(places(1, rest), gated[1][:, rest], gate_rest[:], MULT)
         store(nc.scalar, 1)

@@ -89,7 +89,7 @@ def tile_picked_route2_glusilu_p_kernel(
         for half in halves:
             nc.vector.memset(windows[0][:, half], 0.0)
         nc.scalar.activation(windows[1][:, halves[0]], windows[0][:, halves[0]], SILU)
-        nc.gpsimd.tensor_scalar(windows[1][:, halves[1]], windows[0][:, halves[1]], 1.0, 0.0, MULT, ADD)
+        nc.vector.memset(windows[1][:, halves[1]], 0.0)
 
         xw, xs = {}, {}
 

@@ -21,7 +21,7 @@ P = 128
 PACK = 4
 CHUNK = 128
 GROUP = 256
-PIECES = {"w1": (slice(0, H // 4), slice(H // 4, H)), "w3": (slice(0, H // 2), slice(H // 2, H))}
+PIECES = {"w3": (slice(0, H // 2), slice(H // 2, H))}
 PER_COL = 16
 EARLY = 256
 LATE = 128
@@ -33,8 +33,8 @@ OUT_BANKS = ((7, 0), (5, 2), (3, 7), (0, 4))
 
 
 def load_scale_rows(queues, plane, rows):
-    for q in range(4):
-        queues[q * len(queues) // 4].dma_start(out=plane[32 * q : 32 * q + 4, :].bitcast(I32), in_=rows[4 * q : 4 * q + 4, :].bitcast(I32))
+    for r in range(4):
+        queues[r * len(queues) // 4].dma_start(out=plane[r:P:32, :].bitcast(I32), in_=rows[r:16:4, :].bitcast(I32))
 
 
 def tile_picked_route2_glusilu_p_kernel(
@@ -72,10 +72,12 @@ def tile_picked_route2_glusilu_p_kernel(
         w2s = sbuf("w2s", N, U8)
         nc.vector.memset(xs_table[:].bitcast(I32), 0)
         nc.vector.memset(w2s[:].bitcast(I32), 0)
-        load_weight_piece("w1", w1, 0)
+        raw_w1 = sbuf("raw_w1", PACK * H, F32)
+        w1_rows = w1.rearrange("(p j) c -> p (j c)", j=PACK)
+        nc.sync.dma_start(out=raw_w1[:, :H], in_=w1_rows[:, :H])
         nc.sync.dma_start(offs_sb[:], offs)
-        load_scale_rows((nc.sync, nc.scalar), xs_table, x_scales[0])
-        load_weight_piece("w1", w1, 1)
+        load_scale_rows((nc.sync,), xs_table, x_scales[0])
+        nc.sync.dma_start(out=raw_w1[:, H:], in_=w1_rows[:, H:])
         nc.sync.dma_start(out=xw_table[:].bitcast(I32), in_=x_words[0].rearrange("p c r -> p (c r)").bitcast(I32))
         for c in range(2):
             load_weight_piece("w3", w3, c)
@@ -101,9 +103,9 @@ def tile_picked_route2_glusilu_p_kernel(
 
         gather(xs, xs_table, 0, S, sbuf("xs", S, U8))
 
-        codes, scales, grouped = {}, {}, {}
+        codes, scales = {}, {}
+        grouped = {"w3": sbuf("grouped_w3", H * PACK, BF16)}
         for name in ("w1", "w3"):
-            grouped[name] = sbuf(f"grouped_{name}", H * PACK, BF16)
             codes[name] = sbuf(f"codes_{name}", H, U32)
             scales[name] = sbuf(f"scales_{name}", H, U8)
 
@@ -125,12 +127,28 @@ def tile_picked_route2_glusilu_p_kernel(
                 in_=grouped[name][:, cols.start * PACK : cols.stop * PACK],
             )
 
-        all_tiles = slice(0, PACK)
         tile_pairs = (slice(0, 2), slice(2, PACK))
-        deal(nc.scalar.copy, "w1", 0, all_tiles)
-        for tiles in tile_pairs:
-            deal(nc.scalar.copy, "w1", 1, tiles)
-            quantise("w1", tiles)
+        w1_source = raw_w1[:].rearrange("p (j m t) -> p m j t", j=PACK, t=PACK)
+        w1_pairs = [sbuf(f"grouped_w1_{c}", 2 * P * PACK, BF16) for c in range(2)]
+
+        def deal_w1(copy, c, channels):
+            dealt = w1_pairs[c][:].rearrange("p (t m j) -> p m j t", t=2, j=PACK)
+            copy(dealt[:, channels], w1_source[:, channels, :, tile_pairs[c]])
+
+        def quantise_w1(c, cols):
+            first = 2 * P * c
+            nc.vector.quantize_mx(
+                out=codes["w1"][:, first + cols.start : first + cols.stop].bitcast(FP8X4),
+                scales=scales["w1"][:, first + cols.start : first + cols.stop],
+                in_=w1_pairs[c][:, cols.start * PACK : cols.stop * PACK],
+            )
+
+        deal_w1(nc.scalar.copy, 1, slice(0, P))
+        for first in (0, P // 2):
+            deal_w1(nc.vector.tensor_copy, 0, slice(first, first + P // 2))
+        quantise_w1(1, slice(0, 2 * P))
+        for first in (0, P, P // 2, P + P // 2):
+            quantise_w1(0, slice(first, first + P // 2))
         gather(xw, xw_table, 0, EARLY, sbuf("xw0", EARLY, U32))
         gather(xw, xw_table, EARLY, S - EARLY - LATE, sbuf("xw1", S - EARLY - LATE, U32))
         deal(nc.scalar.copy, "w3", 0, tile_pairs[0])

@@ -143,12 +143,11 @@ def tile_picked_route2_glusilu_p_kernel(
                 in_=w1_pairs[c][:, cols.start * PACK : cols.stop * PACK],
             )
 
-        deal_w1(nc.scalar.copy, 1, slice(0, P))
-        for first in (0, P // 2):
-            deal_w1(nc.vector.tensor_copy, 0, slice(first, first + P // 2))
-        quantise_w1(1, slice(0, 2 * P))
-        for first in (0, P, P // 2, P + P // 2):
-            quantise_w1(0, slice(first, first + P // 2))
+        deal_w1(nc.scalar.copy, 0, slice(0, P))
+        deal_w1(nc.vector.tensor_copy, 1, slice(P // 2, P))
+        deal_w1(nc.scalar.copy, 1, slice(0, P // 2))
+        for c in range(2):
+            quantise_w1(c, slice(0, 2 * P))
         gather(xw, xw_table, 0, EARLY, sbuf("xw0", EARLY, U32))
         gather(xw, xw_table, EARLY, S - EARLY - LATE, sbuf("xw1", S - EARLY - LATE, U32))
         deal(nc.scalar.copy, "w3", 0, tile_pairs[0])

@@ -24,6 +24,7 @@ GROUP = 256
 PIECES = {"w3": (slice(0, H // 2), slice(H // 2, H))}
 PER_COL = 16
 EARLY = 256
+FRONT = 3 * H // 2
 LATE = 128
 SILU_BYTES = CHUNK * PACK * 4
 GROUPS = (slice(0, 256), slice(256, 640), slice(640, 896), slice(896, S))
@@ -32,9 +33,9 @@ LINEAR_BANKS = (5, 6, 1, 2, 3, 4, 6, 1)
 OUT_BANKS = ((7, 0), (5, 2), (3, 7), (0, 4))
 
 
-def load_scale_rows(queues, plane, rows):
-    for r in range(4):
-        queues[r * len(queues) // 4].dma_start(out=plane[r:P:32, :].bitcast(I32), in_=rows[r:16:4, :].bitcast(I32))
+def load_scale_rows(queue, plane, rows, which=range(4)):
+    for r in which:
+        queue.dma_start(out=plane[r:P:32, :].bitcast(I32), in_=rows[r:16:4, :].bitcast(I32))
 
 
 def tile_picked_route2_glusilu_p_kernel(
@@ -74,14 +75,15 @@ def tile_picked_route2_glusilu_p_kernel(
         nc.vector.memset(w2s[:].bitcast(I32), 0)
         raw_w1 = sbuf("raw_w1", PACK * H, F32)
         w1_rows = w1.rearrange("(p j) c -> p (j c)", j=PACK)
-        nc.sync.dma_start(out=raw_w1[:, :H], in_=w1_rows[:, :H])
+        nc.sync.dma_start(out=raw_w1[:, :FRONT], in_=w1_rows[:, :FRONT])
         nc.sync.dma_start(offs_sb[:], offs)
-        load_scale_rows((nc.sync,), xs_table, x_scales[0])
-        nc.sync.dma_start(out=raw_w1[:, H:], in_=w1_rows[:, H:])
+        load_scale_rows(nc.sync, xs_table, x_scales[0])
+        nc.sync.dma_start(out=raw_w1[:, FRONT:], in_=w1_rows[:, FRONT:])
         nc.sync.dma_start(out=xw_table[:].bitcast(I32), in_=x_words[0].rearrange("p c r -> p (c r)").bitcast(I32))
+        load_scale_rows(nc.sync, w2s, w2_scales[0], range(2))
         for c in range(2):
             load_weight_piece("w3", w3, c)
-        load_scale_rows((nc.sync,), w2s, w2_scales[0])
+        load_scale_rows(nc.sync, w2s, w2_scales[0], range(2, 4))
         nc.sync.dma_start(out=w2w[:].bitcast(I32), in_=w2_words[0].rearrange("p c r -> p (c r)").bitcast(I32))
         nc.sync.dma_start(out=gate_first[:], in_=gate[:, :GROUP])
         nc.sync.dma_start(dst_sb[:], dst)
@@ -109,23 +111,25 @@ def tile_picked_route2_glusilu_p_kernel(
             codes[name] = sbuf(f"codes_{name}", H, U32)
             scales[name] = sbuf(f"scales_{name}", H, U8)
 
-        def deal(copy, name, c, tiles):
+        def deal(copy, name, c, tiles, part=slice(0, P // 2)):
             dealt = grouped[name][:].rearrange("p (t m j) -> p m j t", t=PACK, j=PACK)
             source = raw[name, c][:].rearrange("p j (m t) -> p m j t", t=PACK)
             cols = PIECES[name][c]
-            copy(dealt[:, cols.start // PACK : cols.stop // PACK, :, tiles], source[:, :, :, tiles])
+            first = cols.start // PACK
+            copy(dealt[:, first + part.start : first + part.stop, :, tiles], source[:, part, :, tiles])
 
         def gpsimd_cast(target, source):
             order = "p m j t -> p t m j"
             nc.gpsimd.tensor_scalar(target.rearrange(order), source.rearrange(order), 1.0, 0.0, MULT, ADD)
 
-        def quantise(name, tiles):
-            cols = slice(tiles.start * P, tiles.stop * P)
-            nc.vector.quantize_mx(
-                out=codes[name][:, cols].bitcast(FP8X4),
-                scales=scales[name][:, cols],
-                in_=grouped[name][:, cols.start * PACK : cols.stop * PACK],
-            )
+        def quantise(c):
+            for t in range(PACK):
+                cols = slice(t * P + c * P // 2, t * P + (c + 1) * P // 2)
+                nc.vector.quantize_mx(
+                    out=codes["w3"][:, cols].bitcast(FP8X4),
+                    scales=scales["w3"][:, cols],
+                    in_=grouped["w3"][:, cols.start * PACK : cols.stop * PACK],
+                )
 
         tile_pairs = (slice(0, 2), slice(2, PACK))
         w1_source = raw_w1[:].rearrange("p (j m t) -> p m j t", j=PACK, t=PACK)
@@ -151,11 +155,12 @@ def tile_picked_route2_glusilu_p_kernel(
         gather(xw, xw_table, 0, EARLY, sbuf("xw0", EARLY, U32))
         gather(xw, xw_table, EARLY, S - EARLY - LATE, sbuf("xw1", S - EARLY - LATE, U32))
         deal(nc.scalar.copy, "w3", 0, tile_pairs[0])
-        deal(gpsimd_cast, "w3", 0, tile_pairs[1])
+        deal(gpsimd_cast, "w3", 0, tile_pairs[1], slice(P // 4, P // 2))
+        deal(nc.scalar.copy, "w3", 0, tile_pairs[1], slice(0, P // 4))
+        quantise(0)
         for tiles in tile_pairs:
             deal(nc.vector.tensor_copy, "w3", 1, tiles)
-        for tiles in tile_pairs:
-            quantise("w3", tiles)
+        quantise(1)
         gather(xw, xw_table, S - LATE, LATE, sbuf("xw2", LATE, U32, "raw_w3_1"))
 
         def first_product(name, c, bank):

@@ -155,8 +155,8 @@ def tile_picked_route2_glusilu_p_kernel(
         gather(xw, xw_table, 0, EARLY, sbuf("xw0", EARLY, U32))
         gather(xw, xw_table, EARLY, S - EARLY - LATE, sbuf("xw1", S - EARLY - LATE, U32))
         deal(nc.scalar.copy, "w3", 0, tile_pairs[0])
-        deal(gpsimd_cast, "w3", 0, tile_pairs[1], slice(P // 4, P // 2))
-        deal(nc.scalar.copy, "w3", 0, tile_pairs[1], slice(0, P // 4))
+        deal(gpsimd_cast, "w3", 0, tile_pairs[1], slice(P // 8, P // 2))
+        deal(nc.scalar.copy, "w3", 0, tile_pairs[1], slice(0, P // 8))
         quantise(0)
         for tiles in tile_pairs:
             deal(nc.vector.tensor_copy, "w3", 1, tiles)
@@ -259,10 +259,10 @@ def tile_picked_route2_glusilu_p_kernel(
         multiply(2)
         activate(5)
         activate(6)
-        multiply(3, slice(0, CHUNK // 2))
+        multiply(3, slice(0, CHUNK // 4))
         gated_product(0, 0)
         scalar_scatter(0, GROUPS[0])
-        multiply(3, slice(CHUNK // 2, CHUNK))
+        multiply(3, slice(CHUNK // 4, CHUNK))
         multiply(4)
         gated_product(1, 0)
         scalar_scatter(1, GROUPS[0])
@@ -275,11 +275,10 @@ def tile_picked_route2_glusilu_p_kernel(
         multiply(7)
         quantise_hidden(5, 7)
         quantise_hidden(7, 8)
-        plain_product(1)
-        gated_product(0, 2)
-        plain_product(2)
-        plain_product(3)
-        gated_product(0, 3)
+        for g in (1, 2, 3):
+            plain_product(g)
+        for g in (2, 3):
+            gated_product(0, g)
         scalar_scatter(0, slice(GROUPS[2].start, S))
         store(nc.sync, 0)
         rest = slice(GROUP, S)

from contextlib import ExitStack

import concourse.mybir as mybir

K, T, S, H, N, U = 512, 2048, 1024, 512, 256, 2048
FLOPS = 2 * S * (2 * K * H + H * N)

F32 = mybir.dt.float32
BF16 = mybir.dt.bfloat16
I32 = mybir.dt.int32
U32 = mybir.dt.uint32
U16 = mybir.dt.uint16
U8 = mybir.dt.uint8
FP8X4 = mybir.dt.float8_e4m3fn_x4
MULT = mybir.AluOpType.mult
ADD = mybir.AluOpType.add
COPY = mybir.ActivationFunctionType.Copy
SILU = mybir.ActivationFunctionType.Silu

P = 128
PACK = 4
CHUNK = 128
GROUP = 256
PIECES = {"w3": (slice(0, H // 2), slice(H // 2, H))}
PER_COL = 16
EARLY = 256
FRONT = 3 * H // 2
LATE = 128
SILU_BYTES = CHUNK * PACK * 4
GROUPS = (slice(0, 256), slice(256, 640), slice(640, 896), slice(896, S))
SILU_BANKS = (0, 1, 2, 3, 4, 5, 6, 0)
LINEAR_BANKS = (5, 6, 1, 2, 3, 4, 6, 1)
OUT_BANKS = ((7, 0), (5, 2), (3, 7), (0, 4))


def load_scale_rows(queue, plane, rows, which=range(4)):
    for r in which:
        queue.dma_start(out=plane[r:P:32, :].bitcast(I32), in_=rows[r:16:4, :].bitcast(I32))


def tile_picked_route2_glusilu_p_kernel(
    tc, x_words, x_scales, gate, w1, w3, w2_words, w2_scales, offs, dst, out
):
    nc = tc.nc
    with ExitStack() as ctx:
        keep = ctx.enter_context(tc.tile_pool(name="keep", bufs=1))
        psum = ctx.enter_context(tc.psum_pool(name="psum", bufs=1))
        shared = ctx.enter_context(tc.tile_pool(name="shared", bufs=1))

        def sbuf(name, columns, dtype, tag=None):
            return keep.tile([P, columns], dtype, name=name, tag=tag or name, align_bytes=64)

        offs_sb = keep.tile([P, S // PER_COL], U16, name="offs_sb")
        dst_sb = keep.tile([P, S // PER_COL], U16, name="dst_sb")
        xs_table = sbuf("xs_table", T, U8)
        xw_table = sbuf("xw_table", T, U32)
        windows = [sbuf(f"window{m}", U, F32) for m in range(N // P)]

        raw = {}

        def load_weight_piece(name, w, c):
            cols = PIECES[name][c]
            shape = [P, PACK, cols.stop - cols.start]
            if (name, c) == ("w3", 0):
                raw[name, c] = shared.tile(shape, F32, name="raw_w3_0", align_bytes=64, offset=SILU_BYTES - 64)
            else:
                raw[name, c] = keep.tile(shape, F32, name=f"raw_{name}_{c}", tag=f"raw_{name}_{c}", align_bytes=64)
            nc.sync.dma_start(out=raw[name, c][:], in_=w.rearrange("(p j) c -> p j c", j=PACK)[:, :, cols])

        gate_first = sbuf("gate_first", GROUP, F32)
        gate_rest = sbuf("gate_rest", S - GROUP, F32)
        w2w = sbuf("w2w", N, U32)
        w2s = sbuf("w2s", N, U8)
        nc.vector.memset(xs_table[:].bitcast(I32), 0)
        nc.vector.memset(w2s[:].bitcast(I32), 0)
        raw_w1 = sbuf("raw_w1", PACK * H, F32)
        w1_rows = w1.rearrange("(p j) c -> p (j c)", j=PACK)
        nc.sync.dma_start(out=raw_w1[:, :FRONT], in_=w1_rows[:, :FRONT])
        nc.sync.dma_start(offs_sb[:], offs)
        load_scale_rows(nc.sync, xs_table, x_scales[0])
        nc.sync.dma_start(out=raw_w1[:, FRONT:], in_=w1_rows[:, FRONT:])
        nc.sync.dma_start(out=xw_table[:].bitcast(I32), in_=x_words[0].rearrange("p c r -> p (c r)").bitcast(I32))
        load_scale_rows(nc.sync, w2s, w2_scales[0], range(2))
        for c in range(2):
            load_weight_piece("w3", w3, c)
        load_scale_rows(nc.sync, w2s, w2_scales[0], range(2, 4))
        nc.sync.dma_start(out=w2w[:].bitcast(I32), in_=w2_words[0].rearrange("p c r -> p (c r)").bitcast(I32))
        nc.sync.dma_start(out=gate_first[:], in_=gate[:, :GROUP])
        nc.sync.dma_start(dst_sb[:], dst)
        nc.sync.dma_start(out=gate_rest[:], in_=gate[:, GROUP:])

        halves = (slice(0, U // 2), slice(U // 2, U))
        for half in halves:
            nc.vector.memset(windows[0][:, half], 0.0)
        nc.scalar.activation(windows[1][:, halves[0]], windows[0][:, halves[0]], SILU)
        nc.vector.memset(windows[1][:, halves[1]], 0.0)

        xw, xs = {}, {}

        def gather(into, table, first, count, picked):
            cols = slice(first // PER_COL, (first + count) // PER_COL)
            nc.vector.tensor_copy(picked[:], table[:].indirect(offs_sb[:, cols]))
            for c in range(count // CHUNK):
                into[first // CHUNK + c] = picked[:, c * CHUNK : (c + 1) * CHUNK]

        gather(xs, xs_table, 0, S, sbuf("xs", S, U8))

        codes, scales = {}, {}
        grouped = {"w3": sbuf("grouped_w3", H * PACK, BF16)}
        for name in ("w1", "w3"):
            codes[name] = sbuf(f"codes_{name}", H, U32)
            scales[name] = sbuf(f"scales_{name}", H, U8)

        def deal(copy, name, c, tiles, part=slice(0, P // 2)):
            dealt = grouped[name][:].rearrange("p (t m j) -> p m j t", t=PACK, j=PACK)
            source = raw[name, c][:].rearrange("p j (m t) -> p m j t", t=PACK)
            cols = PIECES[name][c]
            first = cols.start // PACK
            copy(dealt[:, first + part.start : first + part.stop, :, tiles], source[:, part, :, tiles])

        def gpsimd_cast(target, source):
            order = "p m j t -> p t m j"
            nc.gpsimd.tensor_scalar(target.rearrange(order), source.rearrange(order), 1.0, 0.0, MULT, ADD)

        def quantise(c):
            for t in range(PACK):
                cols = slice(t * P + c * P // 2, t * P + (c + 1) * P // 2)
                nc.vector.quantize_mx(
                    out=codes["w3"][:, cols].bitcast(FP8X4),
                    scales=scales["w3"][:, cols],
                    in_=grouped["w3"][:, cols.start * PACK : cols.stop * PACK],
                )

        tile_pairs = (slice(0, 2), slice(2, PACK))
        w1_source = raw_w1[:].rearrange("p (j m t) -> p m j t", j=PACK, t=PACK)
        w1_pairs = [sbuf(f"grouped_w1_{c}", 2 * P * PACK, BF16) for c in range(2)]

        def deal_w1(copy, c, channels):
            dealt = w1_pairs[c][:].rearrange("p (t m j) -> p m j t", t=2, j=PACK)
            copy(dealt[:, channels], w1_source[:, channels, :, tile_pairs[c]])

        def quantise_w1(c, cols):
            first = 2 * P * c
            nc.vector.quantize_mx(
                out=codes["w1"][:, first + cols.start : first + cols.stop].bitcast(FP8X4),
                scales=scales["w1"][:, first + cols.start : first + cols.stop],
                in_=w1_pairs[c][:, cols.start * PACK : cols.stop * PACK],
            )

        deal_w1(nc.scalar.copy, 0, slice(0, P))
        deal_w1(nc.vector.tensor_copy, 1, slice(P // 2, P))
        deal_w1(nc.scalar.copy, 1, slice(0, P // 2))
        for c in range(2):
            quantise_w1(c, slice(0, 2 * P))
        gather(xw, xw_table, 0, EARLY, sbuf("xw0", EARLY, U32))
        gather(xw, xw_table, EARLY, S - EARLY - LATE, sbuf("xw1", S - EARLY - LATE, U32))
        deal(nc.scalar.copy, "w3", 0, tile_pairs[0])
        deal(gpsimd_cast, "w3", 0, tile_pairs[1], slice(P // 8, P // 2))
        deal(nc.scalar.copy, "w3", 0, tile_pairs[1], slice(0, P // 8))
        quantise(0)
        for tiles in tile_pairs:
            deal(nc.vector.tensor_copy, "w3", 1, tiles)
        quantise(1)
        gather(xw, xw_table, S - LATE, LATE, sbuf("xw2", LATE, U32, "raw_w3_1"))

        def first_product(name, c, bank):
            acc = psum.tile([P, PACK, CHUNK], F32, name=f"acc_{name}_{c}", tag=f"bank{bank}")
            for t in range(PACK):
                cols = slice(t * P, (t + 1) * P)
                nc.tensor.matmul_mx(
                    out=acc[:, t, :],
                    lhsT=codes[name][:, cols].bitcast(FP8X4),
                    lhsT_scale=scales[name][:, cols],
                    rhs=xw[c].bitcast(FP8X4),
                    rhs_scale=xs[c],
                    start=True,
                    stop=True,
                )
            return acc[:].rearrange("p t n -> p n t")

        wide = CHUNK * PACK
        silu = [shared.tile([P, wide], F32, name=f"silu{c}", align_bytes=64, offset=c * SILU_BYTES)[:] for c in range(2)]
        silu_rest = shared.tile([P, 6 * wide], F32, name="silu_rest", align_bytes=64, offset=2 * SILU_BYTES)
        silu += [silu_rest[:, c * wide : (c + 1) * wide] for c in range(6)]
        hidden = {0: sbuf("hidden_first", 2 * wide, BF16)}
        hw = sbuf("hw", S, U32)
        hs = sbuf("hs", S, U8)
        gated = [sbuf(f"gated{m}", S, F32) for m in range(N // P)]

        y = {}

        def hidden_part(first, last):
            base = max(b for b in hidden if b <= first)
            return hidden[base][:, (first - base) * wide : (last - base) * wide]

        def by_token(ap):
            return ap.rearrange("p (n t) -> p n t", t=PACK)

        def activate(c):
            nc.scalar.activation(by_token(silu[c]), first_product("w1", c, SILU_BANKS[c]), SILU)

        linear = {}

        def multiply(c, tokens=slice(0, CHUNK)):
            if c not in linear:
                linear[c] = first_product("w3", c, LINEAR_BANKS[c])
            target = by_token(hidden_part(c, c + 1))
            nc.vector.tensor_tensor(target[:, tokens], linear[c][:, tokens], by_token(silu[c])[:, tokens], MULT)

        def quantise_hidden(first, last):
            tokens = slice(first * CHUNK, last * CHUNK)
            nc.vector.quantize_mx(out=hw[:, tokens].bitcast(FP8X4), scales=hs[:, tokens], in_=hidden_part(first, last))

        def second_product(m, g):
            group = GROUPS[g]
            cols = slice(m * P, (m + 1) * P)
            y[m, g] = psum.tile([P, group.stop - group.start], F32, name=f"y{m}{g}", tag=f"bank{OUT_BANKS[g][m]}")
            for first in range(group.start, group.stop, GROUP):
                tokens = slice(first, min(first + GROUP, group.stop))
                nc.tensor.matmul_mx(
                    out=y[m, g][:, tokens.start - group.start : tokens.stop - group.start],
                    lhsT=w2w[:, cols].bitcast(FP8X4),
                    lhsT_scale=w2s[:, cols],
                    rhs=hw[:, tokens].bitcast(FP8X4),
                    rhs_scale=hs[:, tokens],
                    start=True,
                    stop=True,
                )

        def gated_product(m, g):
            group = GROUPS[g]
            if (m, g) not in y:
                second_product(m, g)
            weights = gate_rest[:, group.start - GROUP : group.stop - GROUP] if g else gate_first[:]
            nc.vector.tensor_tensor(gated[m][:, group], y[m, g][:], weights, MULT)

        def plain_product(g):
            second_product(1, g)
            nc.vector.tensor_copy(gated[1][:, GROUPS[g]], y[1, g][:])

        def places(m, tokens):
            return windows[m][:].indirect(dst_sb[:, tokens.start // PER_COL : tokens.stop // PER_COL])

        def scalar_scatter(m, tokens):
            nc.scalar.activation(places(m, tokens), gated[m][:, tokens], COPY)

        def store(queue, m):
            queue.dma_start(out=out[m * P : (m + 1) * P, :], in_=windows[m][:])

        for c in range(5):
            activate(c)
        multiply(0)
        multiply(1)
        activate(7)
        quantise_hidden(0, 1)
        quantise_hidden(1, 2)
        second_product(0, 0)
        hidden[2] = shared.tile([P, 3 * wide], BF16, name="hidden_next", align_bytes=64, offset=SILU_BYTES // 2)
        multiply(2)
        activate(5)
        activate(6)
        multiply(3, slice(0, CHUNK // 4))
        gated_product(0, 0)
        scalar_scatter(0, GROUPS[0])
        multiply(3, slice(CHUNK // 4, CHUNK))
        multiply(4)
        gated_product(1, 0)
        scalar_scatter(1, GROUPS[0])
        quantise_hidden(2, 5)
        hidden[5] = sbuf("hidden_late", 3 * wide, BF16, "gate_first")
        multiply(5)
        multiply(6)
        gated_product(0, 1)
        scalar_scatter(0, GROUPS[1])
        multiply(7)
        quantise_hidden(5, 7)
        quantise_hidden(7, 8)
        for g in (1, 2, 3):
            plain_product(g)
        for g in (2, 3):
            gated_product(0, g)
        scalar_scatter(0, slice(GROUPS[2].start, S))
        store(nc.sync, 0)
        rest = slice(GROUP, S)
        nc.vector.tensor_tensor(places(1, rest), gated[1][:, rest], gate_rest[:], MULT)
        store(nc.scalar, 1)
